import numpy as np, ml_dtypes
CORES = [23,119,17,113]
N = 4
import mx_ref
BF = ml_dtypes.bfloat16
def entries(a):
    return np.ascontiguousarray(a.T).reshape(-1)
def table(e):
    return np.ascontiguousarray(np.reshape(e, (-1, 16)).T).astype(np.int32)
def cols(t, e):
    v = np.concatenate([t.reshape(128, -1, 4), np.zeros((128, 1, 4), BF)], axis=1)
    return np.ascontiguousarray(v[:, e]).reshape(128, -1)
def f(rng, *shape):
    return mx_ref.flush((rng.standard_normal(shape, dtype=np.float32) * np.exp2(rng.integers(-2, 3, shape[:-1] + (1,)))).astype(BF))
def wide(rng, *shape, cols=0):
    v = rng.standard_normal(shape, dtype=np.float32) * np.exp2(rng.integers(-12, 13, shape)).astype(np.float32)
    if cols: v *= np.repeat(np.exp2(rng.integers(-cols, cols + 1, shape[:-2] + (1, shape[-1] // 4))) * (rng.random(shape[:-2] + (1, shape[-1] // 4)) > 0.0625), 4, axis=-1).astype(np.float32)
    return mx_ref.flush(v.astype(BF))
P, V, R, O, CAP, ALL = 256, 96, 4, 2, 30, 112
HOME = np.concatenate([np.repeat(np.arange(N), P), np.repeat(np.arange(N), V)])
def flat(a):
    return np.concatenate([entries(e) for e in a])
def game(alt, f1, f2):
    first, second = np.concatenate([np.arange(N * P), f1]), np.concatenate([alt, f2])
    stands = np.where(alt >= 0, np.arange(N * P), -1)
    k, leave, to, out = N * P + np.arange(N * V), np.repeat(np.arange(N), V), f1, []
    for t in range(R):
        was = stands[to]
        stands = np.array(stands); stands[to] = k
        out.append((k, leave, to, stands))
        k, at = was[was >= 0], to[was >= 0]
        leave, to = at // P, np.where(first[k] == at, second[k], first[k])
    return out
def draw(rng, lo, hi, aim):
    stands = np.full((N, P), -1)
    for r in range(N):
        p = rng.permutation(P)[:rng.integers(lo, hi + 1)]
        stands[r, p] = r * P + p
    if aim == "long":
        r = int(rng.integers(0, N)); stands[r] = r * P + np.arange(P)
    if aim == "short": stands[int(rng.integers(0, N))] = -1
    stands = stands.reshape(-1); start = stands >= 0
    first, second = np.concatenate([np.arange(N * P), np.full(N * V, -1)]), np.full(N * P + N * V, -1)
    came, total = np.zeros((N * P + N * V, N), bool), np.zeros((N, N), int)
    k, leave, at = N * P + np.arange(N * V), np.repeat(np.arange(N), V), np.full(N * V, -1)
    goal, last = int(rng.integers(0, N)), None
    mark, late = (goal + 1) % N, 0
    for t in range(R):
        used, free, to = np.zeros((N, N), int), np.ones(N * P, bool), np.full(len(k), -1)
        if aim == "long": mask = stands >= 0
        elif aim == "short" and t > 0: mask = stands < 0
        elif aim == "home" and t == 2: mask = np.isin(np.arange(N * P), last)
        elif aim == "peak": mask = np.arange(N * P) // P == goal
        else: mask = np.ones(N * P, bool)
        known = second[k] >= 0
        o = rng.permutation(len(k))
        if aim == "peak": o = np.concatenate([o[HOME[k[o]] == mark], o[HOME[k[o]] != mark]])
        for i in np.concatenate([o[known[o]], o[~known[o]]]):
            j, q, h = k[i], leave[i], HOME[k[i]]
            good = free & np.repeat((used[q] < CAP) & (came[j] | (total[h] < ALL) | (np.arange(N) == h)), P)
            if at[i] >= 0: good[at[i]] = False
            if known[i]:
                x = second[j] if first[j] == at[i] else first[j]
                if not good[x]: return None
            else:
                if (good & mask).any(): good = good & mask
                if not good.any(): return None
                x = rng.choice(np.flatnonzero(good))
                if t == 0: first[j] = x
                else: second[j] = x
            r = x // P
            to[i] = x; free[x] = False; used[q, r] += 1
            if r != h and not came[j, r]: total[h, r] += 1
            came[j, r] = True
        if aim == "long" and len(k) < N * V: return None
        if aim == "short" and ((t == 1 and len(k) == 0) or (t > 1 and len(k) > 0)): return None
        if aim == "home" and t == R - 1 and (to == k).sum() < N * V // 4: return None
        if aim == "peak" and t < 2 and (used[:, goal] < CAP).any(): return None
        if aim == "peak" and t >= 2: late = max(late, int(used[np.arange(N) != goal, goal].max()))
        was = stands[to]; stands[to] = k; last = to
        k, at = was[was >= 0], to[was >= 0]
        leave = at // P
    if aim == "peak" and (late < CAP - 4 or total[mark, goal] < ALL - 1): return None
    j = np.flatnonzero((second < 0) & np.concatenate([start, np.ones(N * V, bool)]))
    x = rng.integers(0, N * P - 1, len(j)); second[j] = x + (x >= first[j])
    return {"alt": np.stack([table(e) for e in second[:N * P].reshape(N, P)]), "f1": np.stack([table(e) for e in first[N * P:].reshape(N, V)]), "f2": np.stack([table(e) for e in second[N * P:].reshape(N, V)])}
def lists(rng, lo, hi, aim=None):
    for i in range(50):
        d = draw(rng, lo, hi, aim)
        if d is not None: return d
    raise RuntimeError("no draw in 50 tries")
def setup_inputs(rng):
    return {"c": f(rng, N, 128, 4 * P), "v": f(rng, N, 128, 4 * V), "w": f(rng, N, 128, 512 * R * O), **lists(rng, P // 2, 7 * P // 8)}
def setup_inputs_long(rng):
    return {**setup_inputs(rng), **lists(rng, 15 * P // 16, 31 * P // 32, "long")}
def setup_inputs_short(rng):
    return {**setup_inputs(rng), **lists(rng, P // 2, P // 2, "short")}
def setup_inputs_home(rng):
    return {**setup_inputs(rng), **lists(rng, 3 * P // 4, 3 * P // 4, "home")}
def setup_inputs_peak(rng):
    return {**setup_inputs(rng), **lists(rng, 7 * P // 8, 7 * P // 8, "peak")}
def setup_inputs_spread(rng):
    d = setup_inputs(rng); d["c"] = wide(rng, N, 128, 4 * P, cols=6); d["v"] = wide(rng, N, 128, 4 * V, cols=6); return d
def check_inputs(d):
    b = []
    alt, f1, f2 = flat(d["alt"]), flat(d["f1"]), flat(d["f2"])
    if alt.min() < -1 or alt.max() >= N * P or (alt == np.arange(N * P)).any(): b.append("alt")
    if f1.min() < 0 or f1.max() >= N * P: b.append("f1")
    if f2.min() < 0 or f2.max() >= N * P or (f1 == f2).any(): b.append("f2")
    if b: return b
    came = np.zeros((N * P + N * V, N), bool)
    for k, leave, to, stands in game(alt, f1, f2):
        if len(set(to.tolist())) != len(to): return b + ["two columns go to one place in one round"]
        n = np.zeros((N, N), int); np.add.at(n, (leave, to // P), 1)
        if n.max() > CAP: b.append("more than CAP columns from one rank to one rank in one round")
        came[k, to // P] = True
    for q in range(N):
        for r in range(N):
            if q != r and came[HOME == q, r].sum() > ALL: b.append("more than ALL columns of one rank come to another one")
    return b
def reference(c, v, w, alt, f1, f2):
    every = np.concatenate([c[r] for r in range(N)] + [v[r] for r in range(N)], axis=1)
    y = np.zeros((N, 128, R * O * P), np.float32)
    for t, (k, leave, to, stands) in enumerate(game(flat(alt), flat(f1), flat(f2))):
        for r in range(N):
            q = mx_ref.quantize(cols(every, stands[P * r:P * r + P]))
            for i in range(O * t, O * t + O):
                y[r][:, P * i:P * i + P] = mx_ref.matmul(mx_ref.quantize(w[r][:, 512 * i:512 * i + 512]), q)
    return {"y": y}

@@ -1,0 +1,433 @@
+from concourse.bass import DstId, RemoteDMATransfer
+from concourse.mybir import dt, AluOpType as Op, ActivationFunctionType as Act
+
+N, P, V, R, O = 4, 256, 96, 4, 2
+SLOTS = 112
+OWN = SLOTS + V + P
+WIN = OWN + 3 * SLOTS
+ST = 24
+F32, I32, U16, BF, CODE, PL = "float32", "int32", "uint16", "bfloat16", "float8_e4m3fn_x4", "uint8"
+
+
+def _s(n, t):
+    return ("sbuf", [128, n], t)
+
+
+SCRATCH = {
+    "xl": _s(20, I32), "pcol": _s(1, I32), "pci": _s(9, I32), "pcf": _s(9, F32), "pk": _s(8, F32),
+    "k8": _s(8, F32), "pos": _s(8, F32), "ke": _s(8, F32), "xi": _s(120, I32), "xf": _s(48, F32), "ss": _s(14, F32),
+    "land": _s(4 * ST, U16), "lf": _s(4 * ST, F32), "dd": _s(4 * ST, F32), "fri": _s(4 * ST, F32), "fr": _s(4 * ST, F32), "lfo": _s(ST, F32),
+    "eli": _s(88, I32), "el": _s(88, U16), "ex": _s(1408, F32), "tab": _s(3072, F32), "ev": _s(384, F32), "to0": _s(24, F32),
+    "dmi": _s(14, F32), "dum": _s(14, F32), "vai": _s(224, F32), "val": _s(224, F32),
+    "bli": _s(4, F32), "bl": _s(4, U16), "gli": _s(4, F32), "gl": _s(4, U16), "lli": _s(2, F32), "ll": _s(2, U16),
+    "rke": _s(14, F32), "sm": _s(3, F32), "sm8": _s(3, F32), "own14": _s(14, F32), "msk": _s(42, F32), "any1": _s(14, F32), "any2": _s(14, F32),
+    "ein": _s(448, F32), "dix": _s(448, F32), "fst": _s(448, F32), "scs": _s(448, F32), "one": _s(448, F32), "d0": _s(352, F32),
+    "oss": _s(448, F32), "sp": _s(42, F32), "spm": _s(42, F32), "b0a": _s(14, F32), "b0": _s(14, F32), "b1": _s(14, F32),
+    "fo1": _s(3, F32), "fo2": _s(3, F32), "fo3": _s(3, F32), "fof": _s(4, U16), "lst": _s(608, F32),
+    "un": _s(352, F32), "sc": _s(352, F32), "osd": _s(352, F32), "cm": _s(33, F32), "cs1": _s(11, F32), "cs2": _s(11, F32),
+    "fl": _s(11, F32), "bb": _s(11, F32), "fb": _s(11, F32), "of1": _s(11, F32), "ofd": _s(12, U16),
+    "olt": _s(384, F32), "zb": _s(32, F32), "zt": _s(32, F32), "zg": _s(64, F32), "zh": _s(64, F32), "loff": _s(32, U16),
+    "lin": _s(24, U16), "mv": _s(WIN, F32), "m": _s(4 * OWN, F32),
+    "sn": _s(1024, F32), "ts": _s(1024, F32), "idi": _s(32, I32), "idf": _s(32, F32), "ido": _s(32, U16),
+    "mg": _s(512, F32), "om": _s(512, F32), "yb": _s(32, F32), "yt": _s(32, F32), "yg": _s(64, F32), "yh": _s(64, F32), "off": _s(64, U16),
+    "cv": _s(4 * OWN, BF), "qo": _s(OWN, CODE), "qop": _s(OWN, PL), "q": _s(WIN, CODE), "qp": _s(WIN, PL),
+    "wb": _s(4096, BF), "wq": _s(1024, CODE), "wp": _s(1024, PL), "ys": _s(2048, F32),
+    "ps": ("psum", [128, 4096], F32),
+}
+for _t in range(3):
+    SCRATCH["ga%d" % _t] = _s(384, F32)
+    SCRATCH["gt%d" % _t] = _s(384, F32)
+    SCRATCH["ti%d" % (_t + 1)] = _s(24, I32)
+    SCRATCH["to%d" % (_t + 1)] = _s(24, U16)
+    SCRATCH["sq%d" % _t] = _s(SLOTS, CODE)
+    SCRATCH["sqp%d" % _t] = _s(SLOTS, PL)
+for _t in range(4):
+    SCRATCH["k%d" % _t] = _s(P, CODE)
+    SCRATCH["kp%d" % _t] = _s(P, PL)
+PART = {n: ("xi", 20 * k, 20) for k, n in enumerate(["xb", "xc", "xd", "xt", "xp", "rk"])}
+PART.update({n: ("xf", 8 * k, 8) for k, n in enumerate(["emp", "p1", "we", "ne", "z1", "z2"])})
+
+SEMAPHORES = ["sv", "ss", "st", "sg", "ldx", "ldv", "ldc", "ldw0", "ldw1", "arrl", "arrm", "arrq", "arrp", "lsl", "lsm", "lsq", "lsp", "sty"]
+
+
+def rank_program(g, core, T, topo):
+    r = T.rank_of(core)
+    if r is None:
+        return
+    others = [x for x in range(N) if x != r]
+    eng = {"v": g.vector, "s": g.scalar, "t": g.tensor, "g": g, "y": g.sync}
+    sem_of = {"v": "sv", "s": "ss", "t": "st", "g": "sg"}
+    cnt, known, log, total = {}, {k: {} for k in eng}, {}, {}
+
+    def clash(a, b):
+        if a[0] >= b[1] or b[0] >= a[1]:
+            return False
+        return not (a[2] == b[2] and a[2] > 1 and (a[0] - b[0]) % a[2])
+
+    def wait(q, tok):
+        s, v, clock, _ = tok
+        if known[q].get(s, 0) >= v:
+            return
+        eng[q].wait_ge(T.sem[s], v)
+        for k, x in list(clock.items()) + [(s, v)]:
+            known[q][k] = max(known[q].get(k, 0), x)
+
+    def order(q, reads, writes):
+        need = []
+        for regs, w in ((reads, False), (writes, True)):
+            for n, lo, hi, st in regs:
+                for l2, h2, s2, w2, tok in log.get(n, []):
+                    if not (w or w2) or not clash((lo, hi, st), (l2, h2, s2)):
+                        continue
+                    if w and not w2 and tok[3] == q:
+                        continue
+                    need.append(tok)
+        for tok in sorted(need, key=lambda t: -t[1]):
+            wait(q, tok)
+
+    def note(reads, writes, tok):
+        for regs, w in ((reads, False), (writes, True)):
+            for n, lo, hi, st in regs:
+                log.setdefault(n, []).append((lo, hi, st, w, tok))
+
+    def run(q, call, reads, writes):
+        order(q, reads, writes)
+        s = sem_of[q]
+        cnt[s] = cnt.get(s, 0) + 1
+        call(eng[q]).then_inc(T.sem[s], 1)
+        note(reads, writes, (s, cnt[s], dict(known[q]), q))
+
+    def load(q, sem, tot, out, in_, region):
+        eng[q].dma_start(out, in_).then_inc(T.sem[sem], 16)
+        total[sem] = tot
+        note([], [region], (sem, tot, {}, "dma"))
+
+    def ap(x):
+        n, lo, hi, st = x
+        return T[n][:, lo:hi] if st == 1 else T[n][:, lo:hi:st]
+
+    def A(n, lo=0, hi=None, st=1):
+        if n in PART:
+            b, o, w = PART[n]
+            return (b, o + lo, o + (w if hi is None else hi), st)
+        return (n, lo, SCRATCH[n][1][1] if hi is None else hi, st)
+
+    def sc_(x):
+        return ap(x) if isinstance(x, tuple) else x
+
+    def aps(*xs):
+        return [x for x in xs if isinstance(x, tuple)]
+
+    def tt(out, a, b, op):
+        run("v", lambda e: e.tensor_tensor(ap(out), ap(a), ap(b), op), [a, b], [out])
+
+    def ts(out, a, s1, op, s2=None, op1=None):
+        if op1 is None:
+            run("v", lambda e: e.tensor_scalar(ap(out), ap(a), sc_(s1), None, op), [a] + aps(s1), [out])
+        else:
+            run("v", lambda e: e.tensor_scalar(ap(out), ap(a), sc_(s1), sc_(s2), op, op1), [a] + aps(s1, s2), [out])
+
+    def cp(out, a, q="v"):
+        if q == "v":
+            run("v", lambda e: e.tensor_copy(ap(out), ap(a)), [a], [out])
+        else:
+            run("s", lambda e: e.activation(ap(out), ap(a), Act.Copy), [a], [out])
+
+    def tr(out, a):
+        run("v", lambda e: e.transpose(ap(out), ap(a)), [a], [out])
+
+    def fill(out, c):
+        run("v", lambda e: e.memset(ap(out), c), [], [out])
+
+    def gat(out, win, off, q="v"):
+        if q == "v":
+            run("v", lambda e: e.tensor_copy(ap(out), ap(win).indirect(ap(off))), [win, off], [out])
+        else:
+            run("s", lambda e: e.activation(ap(out), ap(win).indirect(ap(off)), Act.Copy), [win, off], [out])
+
+    def sca(win, off, a):
+        run("v", lambda e: e.tensor_copy(ap(win).indirect(ap(off)), ap(a)), [off, a], [win])
+
+    def pick(out, win, off):
+        run("v", lambda e: e.tensor_copy(ap(out).bitcast(dt.uint32), ap(win).bitcast(dt.uint32).indirect(ap(off))), [win, off], [out])
+
+    def quant(c, p, a):
+        run("v", lambda e: e.quantize_mx(ap(c), ap(p), ap(a)), [a], [c, p])
+
+    def iota(out, pattern, base, mult=0):
+        if SCRATCH[out[0]][2] == F32:
+            run("g", lambda e: e.iota(ap(out), pattern, base, mult, allow_small_or_imprecise_dtypes=True), [], [out])
+        else:
+            run("g", lambda e: e.iota(ap(out), pattern, base, mult), [], [out])
+
+    picked, engs = [], {}
+    for x in sorted(others, key=lambda x: len(topo.engines(core, T.cores[x]))):
+        e = [k for k in topo.engines(core, T.cores[x]) if k not in picked][:4]
+        picked += e
+        engs[x] = e
+
+    def post(sem, lsem, srcs, dsts):
+        order("g", srcs, [])
+        trs = []
+        for j, x in enumerate(others):
+            rid, pid, _ = topo.addr(T.cores[x])
+            s, d = ap(srcs[j]), ap(dsts[j])
+            if SCRATCH[srcs[j][0]][2] == CODE:
+                s, d = s.bitcast(dt.uint8), d.bitcast(dt.uint8)
+            trs.append(RemoteDMATransfer(dst_ids=[DstId(rid=rid, pnc=pid)], dma_engine_mask=sum(1 << k for k in engs[x]), remote_sem=T.sem[sem], src=s, dst=d))
+        g.remote_dma_fused(trs, local_sem=T.sem[lsem])
+        total[lsem] = sum(len(engs[x]) for x in others)
+
+    def arrive(sem, regions):
+        total[sem] = 4 * len(others)
+        note([], regions, (sem, 4 * len(others), {}, "far"))
+
+    jobs = []
+    for b in range(4):
+        jobs.append((T.xl[32 * b:32 * b + 32, 8:11], T.f1[:, :]))
+        jobs.append((T.xl[32 * b:32 * b + 32, 14:17], T.f2[:, :]))
+        jobs.append((T.xl[32 * b:32 * b + 32, 0:8], T.alt[:, :]))
+    for n, c in ((T.f1, 11), (T.f2, 17)):
+        for b in range(3):
+            jobs.append((T.xl[32 * b + 16:32 * b + 48, c:c + 3], n[:, :]))
+        jobs.append((T.xl[0:16, c:c + 3], n[8:16, :]))
+        jobs.append((T.xl[112:128, c:c + 3], n[0:8, :]))
+    for k, (o, i) in enumerate(jobs):
+        eng["ys"[k % 2]].dma_start(o, i).then_inc(T.sem.ldx, 16)
+    total["ldx"] = 16 * len(jobs)
+    note([], [A("xl")], ("ldx", 16 * len(jobs), {}, "dma"))
+    load("y", "ldv", 16, T.cv[:, 4 * SLOTS:4 * SLOTS + 4 * V], T.v[:, :], A("cv", 4 * SLOTS, 4 * SLOTS + 4 * V))
+    load("y", "ldc", 16, T.cv[:, 4 * SLOTS + 4 * V:4 * OWN], T.c[:, :], A("cv", 4 * SLOTS + 4 * V, 4 * OWN))
+    for k in range(2):
+        load("y", "ldw%d" % k, 16, T.wb[:, 2048 * k:2048 * k + 2048], T.w[:, 2048 * k:2048 * k + 2048], A("wb", 2048 * k, 2048 * k + 2048))
+
+    iota(A("pcol"), [[0, 1]], 0, 1)
+    iota(A("k8"), [[32, 8]], P * r)
+    iota(A("fri"), [[OWN, 4], [16, ST]], 16)
+    iota(A("dmi"), [[16, 14]], 384)
+    iota(A("vai", 0, 48), [[16, 3], [1, 8], [48, 2]], SLOTS)
+    iota(A("vai", 48, 176), [[16, 8], [1, 8], [128, 2]], SLOTS + V)
+    iota(A("vai", 176, 224), [[16, 3], [1, 8], [48, 2]], SLOTS)
+    iota(A("eli", 0, 64), [[ST, 4], [1, 8], [0, 2]], 12)
+    iota(A("eli", 64, 88), [[ST, 4], [1, 3], [3, 2]], 6)
+    me = ST * r
+    fill(A("land", me + 20, me + 24), 0)
+    for k, (sh, m) in enumerate([(0, 31), (0, 1), (1, 15), (4, 1), (0, 15), (1, 1), (2, 3), (1, 7)]):
+        if sh:
+            ts(A("pci", k, k + 1), A("pcol"), sh, Op.arith_shift_right, m, Op.bitwise_and)
+        else:
+            ts(A("pci", k, k + 1), A("pcol"), m, Op.bitwise_and)
+    cp(A("pcf", 0, 8), A("pci", 0, 8))
+
+    def pf(k):
+        return A("pcf", k, k + 1)
+
+    def pk(k):
+        return A("pk", k, k + 1)
+    ts(A("pos"), A("k8"), pf(0), Op.add)
+    ts(A("ke"), A("k8"), pf(0), Op.add, 1025.0, Op.add)
+    ts(pk(0), pf(1), 128.0, Op.mult, pf(2), Op.add)
+    ts(pk(1), pf(1), 48.0, Op.mult, pf(2), Op.add)
+    ts(pk(3), pf(3), 8.0, Op.mult)
+    ts(pk(4), pf(5), 32.0, Op.mult, pf(6), Op.add)
+    ts(pk(6), pf(1), 32.0, Op.mult, pf(7), Op.add)
+    ts(pk(7), pf(0), 2.5, Op.is_lt)
+    ts(A("pcf", 8, 9), pf(3), -16.0, Op.mult, -40.0, Op.add)
+    ts(pk(5), pf(1), 16.0, Op.mult, pk(4), Op.add)
+    tt(pk(2), A("pcf", 8, 9), pk(1), Op.add)
+
+    ts(A("xb"), A("xl"), 255, Op.bitwise_and)
+    ts(A("xc"), A("xl"), 7, Op.arith_shift_right, 1, Op.bitwise_and)
+    ts(A("emp"), A("xl", 0, 8), 0.0, Op.is_lt)
+    ts(A("xd"), A("xc"), -255.0, Op.mult)
+    tt(A("xt"), A("xl"), A("xb"), Op.add)
+    tt(A("we"), A("emp"), A("ke"), Op.mult)
+    tt(A("xp"), A("xt"), A("xd"), Op.add)
+    tt(A("p1"), A("we"), A("pos"), Op.add)
+    cp(A("land", me, me + 6, 2), A("xp", 8, 11))
+    cp(A("land", me + 1, me + 6, 2), A("xp", 11, 14))
+    tt(A("ss", 0, 6), A("xp", 8, 14), A("xp", 14, 20), Op.add)
+    tt(A("ss", 6, 14), A("xp", 0, 8), A("p1"), Op.add)
+    cp(A("land", me + 6, me + 20), A("ss"))
+    post("arrl", "lsl", [A("land", me, me + ST)] * 3, [A("land", me, me + ST)] * 3)
+    iota(A("lst", 0, 384), [[0, 3], [1, 128]], 0)
+    iota(A("bli"), [[16, 2], [0, 2]], 0)
+    iota(A("lli"), [[8, 2]], 0)
+    iota(A("tab", 1024, 2048), [[2, 1024]], 3072)
+    iota(A("gli"), [[4, 4]], 0)
+    iota(A("mv"), [[1, WIN]], 0)
+
+    q8 = 1.0 / 8192
+    for h in range(4):
+        o = ST * h
+        ts(A("fr", o + 12, o + 20), A("fri", o + 12, o + 20), pk(0), Op.add, q8, Op.mult)
+        ts(A("fr", o + 6, o + 9), A("fri", o + 6, o + 9), pk(1), Op.add, q8, Op.mult)
+        ts(A("fr", o + 9, o + 12), A("fri", o + 9, o + 12), pk(2), Op.add, q8, Op.mult)
+        fill(A("fr", o, o + 6), 0.0)
+        fill(A("fr", o + 20, o + 24), 0.0)
+    own = A("fr", me + 12, me + 20)
+    ts(A("ne"), A("xl", 0, 8), 0.0, Op.is_ge)
+    ts(A("rk"), A("xl"), 8, Op.arith_shift_right)
+    cp(A("lfo"), A("land", me, me + ST))
+    fill(A("ein"), 0.0)
+    tt(A("z1"), own, A("ne"), Op.mult)
+    ts(A("z2"), A("ne"), -OWN * r * q8, Op.mult, OWN * r * q8, Op.add)
+    tt(A("sm"), A("rk", 14, 17), A("rk", 8, 11), Op.is_equal)
+    cp(A("rke", 0, 3), A("rk", 8, 11))
+    cp(A("rke", 3, 11), A("rk", 0, 8))
+    tt(own, A("z1"), A("z2"), Op.add)
+    ts(A("sm8"), A("sm"), 8.0, Op.mult)
+    tt(A("own14", 0, 3), A("lfo", 6, 9), A("fr", me + 6, me + 9), Op.add)
+    tt(A("own14", 11, 14), A("lfo", 6, 9), A("fr", me + 6, me + 9), Op.add)
+    tt(A("rke", 11, 14), A("rk", 14, 17), A("sm8"), Op.subtract)
+    tt(A("own14", 3, 11), A("lfo", 12, 20), own, Op.add)
+    for j, x in enumerate(others):
+        ts(A("msk", 14 * j, 14 * j + 14), A("rke"), float(x), Op.is_equal)
+    m3 = [A("msk", 14 * j, 14 * j + 14) for j in range(3)]
+    tt(A("any1"), m3[0], m3[1], Op.add)
+    for j in range(3):
+        tt(A("ein", j, 448, 32), m3[j], A("own14"), Op.mult)
+    tt(A("any2"), A("any1"), m3[2], Op.add)
+    fill(A("one"), 1.0)
+    tt(A("ein", 3, 448, 32), A("any2"), A("own14"), Op.mult)
+    ts(A("dum"), A("dmi"), pf(4), Op.add)
+    tr(A("dix"), A("ein"))
+    ts(A("val"), A("vai"), pk(3), Op.add)
+    ts(A("fst"), A("dix"), 0.5, Op.is_ge)
+    ts(A("d0"), A("one", 0, 352), pk(7), Op.mult)
+    run("v", lambda e: e.tensor_tensor_scan(ap(A("scs")), ap(A("one")), ap(A("fst")), 0.0, Op.mult, Op.add), [A("one"), A("fst")], [A("scs")])
+    ts(A("bl"), A("bli"), pf(4), Op.add)
+    tr(A("oss"), A("scs"))
+    cp(A("el"), A("eli"))
+    for j in range(3):
+        ts(A("sp", 14 * j, 14 * j + 14), A("oss", j, 448, 32), 128.0 * j - 1.0, Op.add)
+    tt(A("spm"), A("sp"), A("msk"), Op.mult)
+    ts(A("ll"), A("lli"), pk(6), Op.add)
+    ts(A("gl"), A("gli"), pk(5), Op.add)
+    tt(A("b0a"), A("spm", 0, 14), A("spm", 14, 28), Op.add)
+    tt(A("fo1"), A("any2", 0, 3), A("dum", 0, 3), Op.mult)
+    tt(A("b0"), A("b0a"), A("spm", 28, 42), Op.add)
+    tt(A("fo2"), A("dum", 0, 3), A("fo1"), Op.subtract)
+    tt(A("b1"), A("b0"), A("dum"), Op.subtract)
+    tt(A("fo3"), A("b0", 0, 3), A("fo2"), Op.add)
+    fill(A("zb"), 0.0)
+    cp(A("fof", 0, 3), A("fo3"))
+    fill(A("cv", 0, 4 * SLOTS), 0.0)
+    sca(A("lst"), A("fof", 0, 3), A("val", 0, 48))
+    quant(A("qo"), A("qop"), A("cv"))
+    quant(A("q", 0, OWN), A("qp", 0, OWN), A("cv"))
+    for h in range(4):
+        cp(A("m", OWN * h, OWN * h + OWN), A("mv", 0, OWN), "s")
+    cp(A("tab", 2048, 3072), A("tab", 1024, 2048), "s")
+
+    arrive("arrl", [A("land", ST * x, ST * x + ST) for x in others])
+    cp(A("lf"), A("land"))
+    tt(A("dd"), A("lf"), A("fr"), Op.add)
+    gat(A("ex", 512, 1024), A("dd"), A("el", 32, 64), "s")
+    gat(A("ex", 0, 512), A("dd"), A("el", 0, 32))
+    gat(A("ex", 1024, 1408), A("dd"), A("el", 64, 88), "s")
+    tr(A("tab", 0, 512), A("ex", 0, 512))
+    for h in range(4):
+        cp(A("to0", 6 * h, 6 * h + 6), A("lf", ST * h, ST * h + 6), "s")
+    tr(A("tab", 512, 1024), A("ex", 512, 1024))
+    mine = (P * r, P * r + P)
+    first = A("tab", 0, 1024)
+    for h in (2, 3, 0, 1):
+        gat(A("ga0", 96 * h, 96 * h + 96), first, A("land", ST * h, ST * h + 6), "s" if h > 1 else "v")
+    tr(A("ev"), A("ex", 1024, 1408))
+    for t in range(3):
+        if t:
+            gat(A("ga%d" % t, 192, 384), A("tab"), A("to%d" % t, 12, 24), "s")
+            gat(A("ga%d" % t, 0, 192), A("tab"), A("to%d" % t, 0, 12))
+            tr(A("gt%d" % t), A("ga%d" % t))
+            sca(A("tab"), A("to%d" % t), A("ga%d" % (t - 1)))
+        else:
+            tr(A("gt0"), A("ga0"))
+            for h in range(4):
+                sca(first, A("land", ST * h, ST * h + 6), A("ev", 96 * h, 96 * h + 96))
+        cp(A("sn", P * t, P * t + P), A("tab", *mine), "s")
+        tt(A("ti%d" % (t + 1)), A("gt%d" % t, 0, 384, 16), A("ti%d" % t) if t else A("to0"), Op.subtract)
+        cp(A("to%d" % (t + 1)), A("ti%d" % (t + 1)))
+
+    tt(A("un", 0, 256), A("tab", *mine), A("dix", 96, 352), Op.is_equal)
+    fo = A("land", me, me + 6)
+    run("v", lambda e: e.tensor_tensor(ap(A("un", 256, 352)), ap(first).indirect(ap(fo)), ap(A("dix", 352, 448)), Op.is_equal), [first, fo, A("dix", 352, 448)], [A("un", 256, 352)])
+    run("v", lambda e: e.tensor_tensor_scan(ap(A("sc")), ap(A("d0")), ap(A("un")), 0.0, Op.mult, Op.add), [A("d0"), A("un")], [A("sc")])
+    tr(A("osd"), A("sc"))
+    for j in range(3):
+        tt(A("cm", 11 * j, 11 * j + 11), A("osd", j, 352, 32), A("msk", 14 * j + 3, 14 * j + 14), Op.mult)
+    tt(A("fl"), A("any2", 3, 14), A("osd", 3, 352, 32), Op.subtract)
+    tt(A("cs1"), A("cm", 0, 11), A("cm", 11, 22), Op.add)
+    tt(A("bb"), A("b1", 3, 14), A("cm", 22, 33), Op.subtract)
+    tt(A("cs2"), A("bb"), A("cs1"), Op.subtract)
+    tt(A("fb"), A("fl"), A("cs2"), Op.mult)
+    tt(A("of1"), A("fb"), A("dum", 3, 14), Op.add)
+    cp(A("ofd", 0, 11), A("of1"))
+    sca(A("lst"), A("ofd", 0, 11), A("val", 48, 224))
+    tr(A("olt"), A("lst", 0, 384))
+    tt(A("zb", 0, 12), A("olt", 0, 384, 32), A("olt", 16, 384, 32), Op.max)
+    tr(A("zt"), A("zb"))
+    gat(A("zg"), A("zt"), A("bl"))
+    tr(A("zh"), A("zg"))
+    gat(A("loff"), A("zh"), A("ll"))
+    lists = [A("loff", 8 * j, 8 * j + 7) for j in range(3)]
+    at = [sorted(y for y in range(N) if y != x).index(r) for x in others]
+    post("arrm", "lsm", [A("loff", 8 * j, 8 * j + 8) for j in range(3)], [A("lin", 8 * k, 8 * k + 8) for k in at])
+    for j in range(3):
+        pick(A("sq%d" % j), A("qo"), lists[j])
+        gat(A("sqp%d" % j), A("qop"), lists[j], "s")
+    land = [(OWN + SLOTS * k, OWN + SLOTS * k + SLOTS) for k in at]
+    post("arrq", "lsq", [A("sq%d" % j) for j in range(3)], [A("q", *x) for x in land])
+    post("arrp", "lsp", [A("sqp%d" % j) for j in range(3)], [A("qp", *x) for x in land])
+
+    sca(A("tab"), A("to3"), A("ga2"))
+    tr(A("ts", 0, 768), A("sn", 0, 768))
+    tr(A("ts", 768, 1024), A("tab", *mine))
+    cp(A("idi"), A("ts", 0, 1024, 32))
+    quant(A("wq", 0, 512), A("wp", 0, 512), A("wb", 0, 2048))
+    tt(A("idf"), A("ts", 0, 1024, 32), A("idi"), Op.subtract)
+    quant(A("wq", 512, 1024), A("wp", 512, 1024), A("wb", 2048, 4096))
+    ts(A("ido"), A("idf"), 8192.0, Op.mult)
+    arrive("arrm", [A("lin", 8 * k, 8 * k + 8) for k in range(3)])
+    for k, x in enumerate(others):
+        sca(A("m", OWN * x, OWN * x + OWN), A("lin", 8 * k, 8 * k + 7), A("mv", OWN + SLOTS * k, OWN + SLOTS * k + SLOTS))
+    gat(A("mg", 256, 512), A("m"), A("ido", 16, 32), "s")
+    gat(A("mg", 0, 256), A("m"), A("ido", 0, 16))
+    tr(A("om"), A("mg"))
+    cp(A("yb", 0, 16), A("om", 0, 512, 32))
+    cp(A("yb", 16, 32), A("om", 16, 512, 32))
+    tr(A("yt"), A("yb"))
+    gat(A("yg"), A("yt"), A("bl"))
+    tr(A("yh"), A("yg"))
+    gat(A("off"), A("yh"), A("gl"))
+
+    arrive("arrq", [A("q", OWN, WIN)])
+    arrive("arrp", [A("qp", OWN, WIN)])
+
+    def table(t):
+        pick(A("k%d" % t), A("q"), A("off", 16 * t, 16 * t + 16))
+        gat(A("kp%d" % t), A("qp"), A("off", 16 * t, 16 * t + 16), "s")
+        for o in range(O):
+            i = O * t + o
+            wq, wp, kq, kp, z = A("wq", 128 * i, 128 * i + 128), A("wp", 128 * i, 128 * i + 128), A("k%d" % t), A("kp%d" % t), A("ps", 512 * i, 512 * i + P)
+            run("t", lambda e: e.matmul_mx(ap(z), ap(wq), ap(wp), ap(kq), ap(kp), True, True), [wq, wp, kq, kp], [z])
+
+    def out(t):
+        for o in range(O):
+            i = O * t + o
+            for b in range(2):
+                cp(A("ys", P * i + 128 * b, P * i + 128 * b + 128), A("ps", 512 * i + b, 512 * i + P, 2), "vs"[o])
+            reg = A("ys", P * i, P * i + P)
+            order("y", [reg], [])
+            g.sync.dma_start(T.y[:, P * i:P * i + P], ap(reg)).then_inc(T.sem.sty, 16)
+            total["sty"] = total.get("sty", 0) + 16
+    for t in range(R):
+        table(t)
+        if t:
+            out(t - 1)
+    out(R - 1)
+    for q in ("v", "s", "t", "g"):
+        total[sem_of[q]] = cnt[sem_of[q]]
+    for s in SEMAPHORES:
+        if s in total:
+            g.wait_ge(T.sem[s], total[s])

@@ -14,21 +14,21 @@ def _s(n, t):
 
 
 SCRATCH = {
-    "xl": _s(20, I32), "pcol": _s(1, I32), "pci": _s(9, I32), "pcf": _s(9, F32), "pk": _s(8, F32),
+    "xl": _s(20, I32), "pcol": _s(1, I32), "pci": _s(7, I32), "pcf": _s(9, F32), "pk": _s(8, F32), "pkq": _s(3, F32), "lane": _s(1, F32),
     "k8": _s(8, F32), "pos": _s(8, F32), "ke": _s(8, F32), "xi": _s(120, I32), "xf": _s(48, F32), "ss": _s(14, F32),
     "land": _s(4 * ST, U16), "lf": _s(4 * ST, F32), "dd": _s(4 * ST, F32), "fri": _s(4 * ST, F32), "fr": _s(4 * ST, F32), "lfo": _s(ST, F32),
-    "eli": _s(88, I32), "el": _s(88, U16), "ex": _s(1408, F32), "tab": _s(3072, F32), "ev": _s(384, F32), "to0": _s(24, F32),
+    "eli": _s(40, F32), "el": _s(40, U16), "ex": _s(1408, F32), "tab": _s(3072, F32), "ev": _s(384, F32), "to0": _s(24, F32),
     "dmi": _s(14, F32), "dum": _s(14, F32), "vai": _s(224, F32), "val": _s(224, F32),
     "bli": _s(4, F32), "bl": _s(4, U16), "gli": _s(4, F32), "gl": _s(4, U16), "lli": _s(2, F32), "ll": _s(2, U16),
     "rke": _s(14, F32), "sm": _s(3, F32), "sm8": _s(3, F32), "own14": _s(14, F32), "msk": _s(42, F32), "any1": _s(14, F32), "any2": _s(14, F32),
-    "ein": _s(448, F32), "dix": _s(448, F32), "fst": _s(448, F32), "scs": _s(448, F32), "one": _s(448, F32), "d0": _s(352, F32),
-    "oss": _s(448, F32), "sp": _s(42, F32), "spm": _s(42, F32), "b0a": _s(14, F32), "b0": _s(14, F32), "b1": _s(14, F32),
-    "fo1": _s(3, F32), "fo2": _s(3, F32), "fo3": _s(3, F32), "fof": _s(4, U16), "lst": _s(608, F32),
+    "ein": _s(448, F32), "dix": _s(448, F32), "fst": _s(448, F32), "scs": _s(448, F32), "d0": _s(352, F32),
+    "oss": _s(448, F32), "spm": _s(42, F32), "b0a": _s(14, F32), "b0": _s(14, F32), "b1": _s(14, F32),
+    "fo1": _s(3, F32), "fo2": _s(3, F32), "fo3": _s(3, F32), "fof": _s(4, U16), "lst": _s(616, F32),
     "un": _s(352, F32), "sc": _s(352, F32), "osd": _s(352, F32), "cm": _s(33, F32), "cs1": _s(11, F32), "cs2": _s(11, F32),
     "fl": _s(11, F32), "bb": _s(11, F32), "fb": _s(11, F32), "of1": _s(11, F32), "ofd": _s(12, U16),
     "olt": _s(384, F32), "zb": _s(32, F32), "zt": _s(32, F32), "zg": _s(64, F32), "zh": _s(64, F32), "loff": _s(32, U16),
     "lin": _s(24, U16), "mv": _s(WIN, F32), "m": _s(4 * OWN, F32),
-    "sn": _s(1024, F32), "ts": _s(1024, F32), "idi": _s(32, I32), "idf": _s(32, F32), "ido": _s(32, U16),
+    "sn": _s(768, F32), "ts": _s(512, F32), "idi": _s(40, I32), "idf": _s(40, F32), "ido": _s(32, U16),
     "mg": _s(512, F32), "om": _s(512, F32), "yb": _s(32, F32), "yt": _s(32, F32), "yg": _s(64, F32), "yh": _s(64, F32), "off": _s(64, U16),
     "cv": _s(4 * OWN, BF), "qo": _s(OWN, CODE), "qop": _s(OWN, PL), "q": _s(WIN, CODE), "qp": _s(WIN, PL),
     "wb": _s(4096, BF), "wq": _s(1024, CODE), "wp": _s(1024, PL), "ys": _s(2048, F32),
@@ -47,7 +47,7 @@ for _t in range(4):
 PART = {n: ("xi", 20 * k, 20) for k, n in enumerate(["xb", "xc", "xd", "xt", "xp", "rk"])}
 PART.update({n: ("xf", 8 * k, 8) for k, n in enumerate(["emp", "p1", "we", "ne", "z1", "z2"])})
 
-SEMAPHORES = ["sv", "ss", "st", "sg", "ldx", "ldv", "ldc", "ldw0", "ldw1", "arrl", "arrm", "arrq", "arrp", "lsl", "lsm", "lsq", "lsp", "sty"]
+SEMAPHORES = ["sv", "ss", "st", "sg", "ldx", "ldv", "ldc", "ldw0", "ldw1", "arrl", "arrm", "arrq", "arrp", "lsl", "lsm", "lsq", "lsp", "sty", "own", "sns"]
 
 
 def rank_program(g, core, T, topo):
@@ -133,8 +133,14 @@ def rank_program(g, core, T, topo):
         else:
             run("s", lambda e: e.activation(ap(out), ap(a), Act.Copy), [a], [out])
 
+    def act(out, a, scale, bias=0.0):
+        run("s", lambda e: e.activation(ap(out), ap(a), Act.Identity, bias=sc_(bias), scale=sc_(scale)), [a] + aps(scale, bias), [out])
+
     def tr(out, a):
         run("v", lambda e: e.transpose(ap(out), ap(a)), [a], [out])
+
+    def scan(out, a, b, start, op0, op1):
+        run("v", lambda e: e.tensor_tensor_scan(ap(out), ap(a), ap(b), sc_(start), op0, op1), [a, b] + aps(start), [out])
 
     def fill(out, c):
         run("v", lambda e: e.memset(ap(out), c), [], [out])
@@ -203,21 +209,22 @@ def rank_program(g, core, T, topo):
 
     iota(A("pcol"), [[0, 1]], 0, 1)
     iota(A("k8"), [[32, 8]], P * r)
+    iota(A("eli", 0, 16), [[ST, 4], [2, 4]], 12)
+    iota(A("eli", 16, 40), [[ST, 4], [1, 3], [3, 2]], 6)
+    iota(A("bli"), [[16, 2], [0, 2]], 0)
+    iota(A("lli"), [[8, 2]], 0)
+    iota(A("gli"), [[1, 2], [32, 2]], 0)
     iota(A("fri"), [[OWN, 4], [16, ST]], 16)
-    iota(A("dmi"), [[16, 14]], 384)
-    iota(A("vai", 0, 48), [[16, 3], [1, 8], [48, 2]], SLOTS)
-    iota(A("vai", 48, 176), [[16, 8], [1, 8], [128, 2]], SLOTS + V)
-    iota(A("vai", 176, 224), [[16, 3], [1, 8], [48, 2]], SLOTS)
-    iota(A("eli", 0, 64), [[ST, 4], [1, 8], [0, 2]], 12)
-    iota(A("eli", 64, 88), [[ST, 4], [1, 3], [3, 2]], 6)
+    iota(A("dmi"), [[16, 14]], 385)
     me = ST * r
+    q8 = 1.0 / 8192
     fill(A("land", me + 20, me + 24), 0)
-    for k, (sh, m) in enumerate([(0, 31), (0, 1), (1, 15), (4, 1), (0, 15), (1, 1), (2, 3), (1, 7)]):
+    for k, (sh, m) in enumerate([(0, 31), (0, 1), (1, 15), (4, 1), (0, 15), (1, 7), (3, 1)]):
         if sh:
             ts(A("pci", k, k + 1), A("pcol"), sh, Op.arith_shift_right, m, Op.bitwise_and)
         else:
             ts(A("pci", k, k + 1), A("pcol"), m, Op.bitwise_and)
-    cp(A("pcf", 0, 8), A("pci", 0, 8))
+    cp(A("pcf", 0, 7), A("pci", 0, 7))
 
     def pf(k):
         return A("pcf", k, k + 1)
@@ -228,13 +235,27 @@ def rank_program(g, core, T, topo):
     ts(A("ke"), A("k8"), pf(0), Op.add, 1025.0, Op.add)
     ts(pk(0), pf(1), 128.0, Op.mult, pf(2), Op.add)
     ts(pk(1), pf(1), 48.0, Op.mult, pf(2), Op.add)
-    ts(pk(3), pf(3), 8.0, Op.mult)
-    ts(pk(4), pf(5), 32.0, Op.mult, pf(6), Op.add)
-    ts(pk(6), pf(1), 32.0, Op.mult, pf(7), Op.add)
-    ts(pk(7), pf(0), 2.5, Op.is_lt)
     ts(A("pcf", 8, 9), pf(3), -16.0, Op.mult, -40.0, Op.add)
-    ts(pk(5), pf(1), 16.0, Op.mult, pk(4), Op.add)
+    ts(pk(6), pf(1), 32.0, Op.mult, pf(5), Op.add)
     tt(pk(2), A("pcf", 8, 9), pk(1), Op.add)
+    ts(pk(3), pf(3), 8.0, Op.mult)
+    ts(pk(5), pf(1), 15.0, Op.mult, pf(4), Op.add)
+    ts(A("pkq"), A("pk", 0, 3), q8, Op.mult)
+    fill(A("ein"), 0.0)
+    ts(pk(7), pf(0), 10.0, Op.is_lt)
+    ts(A("lane"), pf(0), 32.0, Op.mult)
+    ts(A("el", 0, 16), A("eli", 0, 16), pf(6), Op.add)
+    cp(A("el", 16, 40), A("eli", 16, 40))
+    ts(A("bl"), A("bli"), pf(4), Op.add)
+    ts(A("ll"), A("lli"), pk(6), Op.add)
+    ts(A("gl"), A("gli"), pk(5), Op.add)
+    act(A("fr"), A("fri"), q8)
+    for h in range(4):
+        for k, (a, b) in enumerate(((12, 20), (6, 9), (9, 12))):
+            act(A("fr", ST * h + a, ST * h + b), A("fri", ST * h + a, ST * h + b), q8, A("pkq", k, k + 1))
+    act(A("dum"), A("dmi"), 1.0, pf(4))
+    for a in (0, 256, 512, 768):
+        act(A("ex", a, a + 256), A("ein", 0, 256), 0.0)
 
     ts(A("xb"), A("xl"), 255, Op.bitwise_and)
     ts(A("xc"), A("xl"), 7, Op.arith_shift_right, 1, Op.bitwise_and)
@@ -250,26 +271,17 @@ def rank_program(g, core, T, topo):
     tt(A("ss", 6, 14), A("xp", 0, 8), A("p1"), Op.add)
     cp(A("land", me + 6, me + 20), A("ss"))
     post("arrl", "lsl", [A("land", me, me + ST)] * 3, [A("land", me, me + ST)] * 3)
-    iota(A("lst", 0, 384), [[0, 3], [1, 128]], 0)
-    iota(A("bli"), [[16, 2], [0, 2]], 0)
-    iota(A("lli"), [[8, 2]], 0)
+    iota(A("vai", 0, 48), [[16, 3], [1, 8], [48, 2]], SLOTS)
+    iota(A("vai", 48, 176), [[16, 8], [1, 8], [128, 2]], SLOTS + V)
+    iota(A("vai", 176, 224), [[16, 3], [1, 8], [48, 2]], SLOTS)
+    iota(A("lst", 1, 385), [[0, 3], [1, 128]], 0)
     iota(A("tab", 1024, 2048), [[2, 1024]], 3072)
-    iota(A("gli"), [[4, 4]], 0)
     iota(A("mv"), [[1, WIN]], 0)
 
-    q8 = 1.0 / 8192
-    for h in range(4):
-        o = ST * h
-        ts(A("fr", o + 12, o + 20), A("fri", o + 12, o + 20), pk(0), Op.add, q8, Op.mult)
-        ts(A("fr", o + 6, o + 9), A("fri", o + 6, o + 9), pk(1), Op.add, q8, Op.mult)
-        ts(A("fr", o + 9, o + 12), A("fri", o + 9, o + 12), pk(2), Op.add, q8, Op.mult)
-        fill(A("fr", o, o + 6), 0.0)
-        fill(A("fr", o + 20, o + 24), 0.0)
     own = A("fr", me + 12, me + 20)
     ts(A("ne"), A("xl", 0, 8), 0.0, Op.is_ge)
     ts(A("rk"), A("xl"), 8, Op.arith_shift_right)
     cp(A("lfo"), A("land", me, me + ST))
-    fill(A("ein"), 0.0)
     tt(A("z1"), own, A("ne"), Op.mult)
     ts(A("z2"), A("ne"), -OWN * r * q8, Op.mult, OWN * r * q8, Op.add)
     tt(A("sm"), A("rk", 14, 17), A("rk", 8, 11), Op.is_equal)
@@ -286,46 +298,42 @@ def rank_program(g, core, T, topo):
     m3 = [A("msk", 14 * j, 14 * j + 14) for j in range(3)]
     tt(A("any1"), m3[0], m3[1], Op.add)
     for j in range(3):
-        tt(A("ein", j, 448, 32), m3[j], A("own14"), Op.mult)
+        tt(A("ein", 4 * j, 448, 32), m3[j], A("own14"), Op.mult)
     tt(A("any2"), A("any1"), m3[2], Op.add)
-    fill(A("one"), 1.0)
-    tt(A("ein", 3, 448, 32), A("any2"), A("own14"), Op.mult)
-    ts(A("dum"), A("dmi"), pf(4), Op.add)
-    tr(A("dix"), A("ein"))
-    ts(A("val"), A("vai"), pk(3), Op.add)
-    ts(A("fst"), A("dix"), 0.5, Op.is_ge)
-    ts(A("d0"), A("one", 0, 352), pk(7), Op.mult)
-    run("v", lambda e: e.tensor_tensor_scan(ap(A("scs")), ap(A("one")), ap(A("fst")), 0.0, Op.mult, Op.add), [A("one"), A("fst")], [A("scs")])
-    ts(A("bl"), A("bli"), pf(4), Op.add)
-    tr(A("oss"), A("scs"))
-    cp(A("el"), A("eli"))
-    for j in range(3):
-        ts(A("sp", 14 * j, 14 * j + 14), A("oss", j, 448, 32), 128.0 * j - 1.0, Op.add)
-    tt(A("spm"), A("sp"), A("msk"), Op.mult)
-    ts(A("ll"), A("lli"), pk(6), Op.add)
-    ts(A("gl"), A("gli"), pk(5), Op.add)
-    tt(A("b0a"), A("spm", 0, 14), A("spm", 14, 28), Op.add)
-    tt(A("fo1"), A("any2", 0, 3), A("dum", 0, 3), Op.mult)
-    tt(A("b0"), A("b0a"), A("spm", 28, 42), Op.add)
-    tt(A("fo2"), A("dum", 0, 3), A("fo1"), Op.subtract)
-    tt(A("b1"), A("b0"), A("dum"), Op.subtract)
-    tt(A("fo3"), A("b0", 0, 3), A("fo2"), Op.add)
     fill(A("zb"), 0.0)
-    cp(A("fof", 0, 3), A("fo3"))
+    tt(A("ein", 12, 448, 32), A("any2"), A("own14"), Op.mult)
     fill(A("cv", 0, 4 * SLOTS), 0.0)
-    sca(A("lst"), A("fof", 0, 3), A("val", 0, 48))
+    tr(A("dix"), A("ein"))
+    run("s", lambda e: e.activation(ap(A("fst")), ap(A("dix")), Act.Sign), [A("dix")], [A("fst")])
+    act(A("val"), A("vai"), 1.0, pk(3))
+    act(A("d0"), A("lst", 1, 353), 0.0, pk(7))
     quant(A("qo"), A("qop"), A("cv"))
-    quant(A("q", 0, OWN), A("qp", 0, OWN), A("cv"))
-    for h in range(4):
-        cp(A("m", OWN * h, OWN * h + OWN), A("mv", 0, OWN), "s")
-    cp(A("tab", 2048, 3072), A("tab", 1024, 2048), "s")
+    tt(A("fo1"), A("any2", 0, 3), A("dum", 0, 3), Op.mult)
+    scan(A("scs"), A("fst"), A("fst"), A("lane"), Op.add, Op.max)
+    tr(A("oss"), A("scs"))
+    tt(A("fo2"), A("dum", 0, 3), A("fo1"), Op.subtract)
+    for j in range(3):
+        tt(A("spm", 14 * j, 14 * j + 14), A("oss", 4 * j, 448, 32), m3[j], Op.mult)
+    tt(A("b0a"), A("spm", 0, 14), A("spm", 14, 28), Op.add)
+    tt(A("b0"), A("b0a"), A("spm", 28, 42), Op.add)
+    tt(A("fo3"), A("b0", 0, 3), A("fo2"), Op.add)
+    tt(A("b1"), A("b0"), A("dum"), Op.subtract)
+    cp(A("fof", 0, 3), A("fo3"))
+    sca(A("lst"), A("fof", 0, 3), A("val", 0, 48))
+    quant(A("wq", 0, 512), A("wp", 0, 512), A("wb", 0, 2048))
+    quant(A("wq", 512, 1024), A("wp", 512, 1024), A("wb", 2048, 4096))
+    order("y", [A("qo"), A("qop")], [])
+    g.sync.dma_start(T.q[:, 0:OWN].bitcast(dt.uint8), T.qo[:, 0:OWN].bitcast(dt.uint8)).then_inc(T.sem.own, 16)
+    g.sync.dma_start(T.qp[:, 0:OWN], T.qop[:, 0:OWN]).then_inc(T.sem.own, 16)
+    total["own"] = 32
+    note([], [A("q", 0, OWN), A("qp", 0, OWN)], ("own", 32, {}, "dma"))
 
     arrive("arrl", [A("land", ST * x, ST * x + ST) for x in others])
     cp(A("lf"), A("land"))
     tt(A("dd"), A("lf"), A("fr"), Op.add)
-    gat(A("ex", 512, 1024), A("dd"), A("el", 32, 64), "s")
-    gat(A("ex", 0, 512), A("dd"), A("el", 0, 32))
-    gat(A("ex", 1024, 1408), A("dd"), A("el", 64, 88), "s")
+    gat(A("ex", 512, 1024, 4), A("dd"), A("el", 8, 16), "s")
+    gat(A("ex", 0, 512, 4), A("dd"), A("el", 0, 8))
+    gat(A("ex", 1024, 1408), A("dd"), A("el", 16, 40), "s")
     tr(A("tab", 0, 512), A("ex", 0, 512))
     for h in range(4):
         cp(A("to0", 6 * h, 6 * h + 6), A("lf", ST * h, ST * h + 6), "s")
@@ -335,6 +343,7 @@ def rank_program(g, core, T, topo):
     for h in (2, 3, 0, 1):
         gat(A("ga0", 96 * h, 96 * h + 96), first, A("land", ST * h, ST * h + 6), "s" if h > 1 else "v")
     tr(A("ev"), A("ex", 1024, 1408))
+    cp(A("tab", 2048, 3072), A("tab", 1024, 2048), "s")
     for t in range(3):
         if t:
             gat(A("ga%d" % t, 192, 384), A("tab"), A("to%d" % t, 12, 24), "s")
@@ -345,18 +354,27 @@ def rank_program(g, core, T, topo):
             tr(A("gt0"), A("ga0"))
             for h in range(4):
                 sca(first, A("land", ST * h, ST * h + 6), A("ev", 96 * h, 96 * h + 96))
+        if t < 2:
+            for h in (2 * t, 2 * t + 1):
+                cp(A("m", OWN * h, OWN * h + OWN), A("mv", 0, OWN), "s")
         cp(A("sn", P * t, P * t + P), A("tab", *mine), "s")
+        if t:
+            order("y", [A("sn", P * t, P * t + P)], [A("sn", 0, P)])
+            for p in range(8 * t, 128, 32):
+                g.sync.dma_start(T.sn[p:p + 1, 0:P], T.sn[p:p + 1, P * t:P * t + P]).then_inc(T.sem.sns, 16)
+                total["sns"] = total.get("sns", 0) + 16
         tt(A("ti%d" % (t + 1)), A("gt%d" % t, 0, 384, 16), A("ti%d" % t) if t else A("to0"), Op.subtract)
         cp(A("to%d" % (t + 1)), A("ti%d" % (t + 1)))
+    note([A("sn", P, 3 * P)], [A("sn", 0, P)], ("sns", total["sns"], {}, "dma"))
 
     tt(A("un", 0, 256), A("tab", *mine), A("dix", 96, 352), Op.is_equal)
     fo = A("land", me, me + 6)
     run("v", lambda e: e.tensor_tensor(ap(A("un", 256, 352)), ap(first).indirect(ap(fo)), ap(A("dix", 352, 448)), Op.is_equal), [first, fo, A("dix", 352, 448)], [A("un", 256, 352)])
-    run("v", lambda e: e.tensor_tensor_scan(ap(A("sc")), ap(A("d0")), ap(A("un")), 0.0, Op.mult, Op.add), [A("d0"), A("un")], [A("sc")])
+    scan(A("sc"), A("d0"), A("un"), 0.0, Op.mult, Op.add)
     tr(A("osd"), A("sc"))
     for j in range(3):
-        tt(A("cm", 11 * j, 11 * j + 11), A("osd", j, 352, 32), A("msk", 14 * j + 3, 14 * j + 14), Op.mult)
-    tt(A("fl"), A("any2", 3, 14), A("osd", 3, 352, 32), Op.subtract)
+        tt(A("cm", 11 * j, 11 * j + 11), A("osd", 4 * j, 352, 32), A("msk", 14 * j + 3, 14 * j + 14), Op.mult)
+    tt(A("fl"), A("any2", 3, 14), A("osd", 12, 352, 32), Op.subtract)
     tt(A("cs1"), A("cm", 0, 11), A("cm", 11, 22), Op.add)
     tt(A("bb"), A("b1", 3, 14), A("cm", 22, 33), Op.subtract)
     tt(A("cs2"), A("bb"), A("cs1"), Op.subtract)
@@ -364,7 +382,7 @@ def rank_program(g, core, T, topo):
     tt(A("of1"), A("fb"), A("dum", 3, 14), Op.add)
     cp(A("ofd", 0, 11), A("of1"))
     sca(A("lst"), A("ofd", 0, 11), A("val", 48, 224))
-    tr(A("olt"), A("lst", 0, 384))
+    tr(A("olt"), A("lst", 1, 385))
     tt(A("zb", 0, 12), A("olt", 0, 384, 32), A("olt", 16, 384, 32), Op.max)
     tr(A("zt"), A("zb"))
     gat(A("zg"), A("zt"), A("bl"))
@@ -381,13 +399,14 @@ def rank_program(g, core, T, topo):
     post("arrp", "lsp", [A("sqp%d" % j) for j in range(3)], [A("qp", *x) for x in land])
 
     sca(A("tab"), A("to3"), A("ga2"))
-    tr(A("ts", 0, 768), A("sn", 0, 768))
-    tr(A("ts", 768, 1024), A("tab", *mine))
-    cp(A("idi"), A("ts", 0, 1024, 32))
-    quant(A("wq", 0, 512), A("wp", 0, 512), A("wb", 0, 2048))
-    tt(A("idf"), A("ts", 0, 1024, 32), A("idi"), Op.subtract)
-    quant(A("wq", 512, 1024), A("wp", 512, 1024), A("wb", 2048, 4096))
-    ts(A("ido"), A("idf"), 8192.0, Op.mult)
+    tr(A("ts", 0, 256), A("sn", 0, 256))
+    tr(A("ts", 256, 512), A("tab", *mine))
+    cp(A("idi", 0, 32), A("ts", 0, 256, 8))
+    cp(A("idi", 32, 40), A("ts", 256, 512, 32))
+    tt(A("idf", 0, 32), A("ts", 0, 256, 8), A("idi", 0, 32), Op.subtract)
+    tt(A("idf", 32, 40), A("ts", 256, 512, 32), A("idi", 32, 40), Op.subtract)
+    ts(A("ido"), A("idf", 0, 32), 8192.0, Op.mult)
+    ts(A("ido", 3, 32, 4), A("idf", 32, 40), 8192.0, Op.mult)
     arrive("arrm", [A("lin", 8 * k, 8 * k + 8) for k in range(3)])
     for k, x in enumerate(others):
         sca(A("m", OWN * x, OWN * x + OWN), A("lin", 8 * k, 8 * k + 7), A("mv", OWN + SLOTS * k, OWN + SLOTS * k + SLOTS))

@@ -6,6 +6,8 @@ SLOTS = 112
 OWN = SLOTS + V + P
 WIN = OWN + 3 * SLOTS
 ST = 24
+FLAG = 2
+PLACES = 3072
 F32, I32, U16, BF, CODE, PL = "float32", "int32", "uint16", "bfloat16", "float8_e4m3fn_x4", "uint8"
 
 
@@ -14,12 +16,14 @@ def _s(n, t):
 
 
 SCRATCH = {
-    "xl": _s(20, I32), "pcol": _s(1, I32), "pci": _s(7, I32), "pcf": _s(9, F32), "pk": _s(8, F32), "pkq": _s(3, F32), "lane": _s(1, F32),
+    "xl": _s(20, I32), "pcol": _s(1, I32), "pci": _s(7, I32), "pcf": _s(9, F32), "pk": _s(8, F32), "lane": _s(1, F32),
     "k8": _s(8, F32), "pos": _s(8, F32), "ke": _s(8, F32), "xi": _s(120, I32), "xf": _s(48, F32), "ss": _s(14, F32),
-    "land": _s(4 * ST, U16), "lf": _s(4 * ST, F32), "dd": _s(4 * ST, F32), "fri": _s(4 * ST, F32), "fr": _s(4 * ST, F32), "lfo": _s(ST, F32),
-    "eli": _s(40, F32), "el": _s(40, U16), "ex": _s(1408, F32), "tab": _s(3072, F32), "ev": _s(384, F32), "to0": _s(24, F32),
+    "land": _s(4 * ST, U16), "dd": _s(8 * ST, F32), "fri": _s(4 * ST, F32),
+    "eli": _s(92, F32), "el": _s(92, U16), "ex": _s(1408, F32), "tab": _s(PLACES + 384, F32), "ev": _s(384, F32), "to0": _s(24, F32), "tou": _s(24, U16),
+    "gc": _s(384, F32), "mxi": _s(24, F32), "mx": _s(24, F32), "x2": _s(24, F32), "y2": _s(24, F32), "lcf": _s(24, F32), "lc": _s(24, U16), "w1": _s(24, F32),
+    "ne3": _s(16, F32), "df3": _s(16, F32), "pr3": _s(16, F32), "r3": _s(16, F32),
     "dmi": _s(14, F32), "dum": _s(14, F32), "vai": _s(224, F32), "val": _s(224, F32),
-    "bli": _s(4, F32), "bl": _s(4, U16), "gli": _s(4, F32), "gl": _s(4, U16), "lli": _s(2, F32), "ll": _s(2, U16),
+    "bli": _s(4, F32), "bl": _s(4, U16), "lli": _s(2, F32), "ll": _s(2, U16),
     "rke": _s(14, F32), "sm": _s(3, F32), "sm8": _s(3, F32), "own14": _s(14, F32), "msk": _s(42, F32), "any1": _s(14, F32), "any2": _s(14, F32),
     "ein": _s(448, F32), "dix": _s(448, F32), "fst": _s(448, F32), "scs": _s(448, F32), "d0": _s(352, F32),
     "oss": _s(448, F32), "spm": _s(42, F32), "b0a": _s(14, F32), "b0": _s(14, F32), "b1": _s(14, F32),
@@ -28,16 +32,15 @@ SCRATCH = {
     "fl": _s(11, F32), "bb": _s(11, F32), "fb": _s(11, F32), "of1": _s(11, F32), "ofd": _s(12, U16),
     "olt": _s(384, F32), "zb": _s(32, F32), "zt": _s(32, F32), "zg": _s(64, F32), "zh": _s(64, F32), "loff": _s(32, U16),
     "lin": _s(24, U16), "mv": _s(WIN, F32), "m": _s(4 * OWN, F32),
-    "sn": _s(768, F32), "ts": _s(512, F32), "idi": _s(40, I32), "idf": _s(40, F32), "ido": _s(32, U16),
-    "mg": _s(512, F32), "om": _s(512, F32), "yb": _s(32, F32), "yt": _s(32, F32), "yg": _s(64, F32), "yh": _s(64, F32), "off": _s(64, U16),
+    "sn": _s(768, F32), "ts": _s(256, F32), "ido": _s(64, U16), "mg": _s(1024, F32), "om": _s(1024, F32), "off": _s(64, U16),
     "cv": _s(4 * OWN, BF), "qo": _s(OWN, CODE), "qop": _s(OWN, PL), "q": _s(WIN, CODE), "qp": _s(WIN, PL),
     "wb": _s(4096, BF), "wq": _s(1024, CODE), "wp": _s(1024, PL), "ys": _s(2048, F32),
+    "ga0": _s(384, F32), "ga2": _s(384, F32),
     "ps": ("psum", [128, 4096], F32),
 }
 for _t in range(3):
-    SCRATCH["ga%d" % _t] = _s(384, F32)
     SCRATCH["gt%d" % _t] = _s(384, F32)
-    SCRATCH["ti%d" % (_t + 1)] = _s(24, I32)
+    SCRATCH["ti%d" % (_t + 1)] = _s(24, F32)
     SCRATCH["to%d" % (_t + 1)] = _s(24, U16)
     SCRATCH["sq%d" % _t] = _s(SLOTS, CODE)
     SCRATCH["sqp%d" % _t] = _s(SLOTS, PL)
@@ -46,6 +49,7 @@ for _t in range(4):
     SCRATCH["kp%d" % _t] = _s(P, PL)
 PART = {n: ("xi", 20 * k, 20) for k, n in enumerate(["xb", "xc", "xd", "xt", "xp", "rk"])}
 PART.update({n: ("xf", 8 * k, 8) for k, n in enumerate(["emp", "p1", "we", "ne", "z1", "z2"])})
+PART.update({"ga1": ("tab", PLACES, 384), "lf": ("dd", 0, 4 * ST), "fr": ("dd", 4 * ST, 4 * ST)})
 
 SEMAPHORES = ["sv", "ss", "st", "sg", "ldx", "ldv", "ldc", "ldw0", "ldw1", "arrl", "arrm", "arrq", "arrp", "lsl", "lsm", "lsq", "lsp", "sty", "own", "sns"]
 
@@ -90,12 +94,12 @@ def rank_program(g, core, T, topo):
             for n, lo, hi, st in regs:
                 log.setdefault(n, []).append((lo, hi, st, w, tok))
 
-    def run(q, call, reads, writes):
+    def run(q, call, reads, writes, listed=False):
         order(q, reads, writes)
         s = sem_of[q]
         cnt[s] = cnt.get(s, 0) + 1
         call(eng[q]).then_inc(T.sem[s], 1)
-        note(reads, writes, (s, cnt[s], dict(known[q]), q))
+        note(reads, writes, (s, cnt[s], dict(known[q]), "list" if listed else q))
 
     def load(q, sem, tot, out, in_, region):
         eng[q].dma_start(out, in_).then_inc(T.sem[sem], 16)
@@ -147,15 +151,15 @@ def rank_program(g, core, T, topo):
 
     def gat(out, win, off, q="v"):
         if q == "v":
-            run("v", lambda e: e.tensor_copy(ap(out), ap(win).indirect(ap(off))), [win, off], [out])
+            run("v", lambda e: e.tensor_copy(ap(out), ap(win).indirect(ap(off))), [win, off], [out], True)
         else:
-            run("s", lambda e: e.activation(ap(out), ap(win).indirect(ap(off)), Act.Copy), [win, off], [out])
+            run("s", lambda e: e.activation(ap(out), ap(win).indirect(ap(off)), Act.Copy), [win, off], [out], True)
 
     def sca(win, off, a):
         run("v", lambda e: e.tensor_copy(ap(win).indirect(ap(off)), ap(a)), [off, a], [win])
 
     def pick(out, win, off):
-        run("v", lambda e: e.tensor_copy(ap(out).bitcast(dt.uint32), ap(win).bitcast(dt.uint32).indirect(ap(off))), [win, off], [out])
+        run("v", lambda e: e.tensor_copy(ap(out).bitcast(dt.uint32), ap(win).bitcast(dt.uint32).indirect(ap(off))), [win, off], [out], True)
 
     def quant(c, p, a):
         run("v", lambda e: e.quantize_mx(ap(c), ap(p), ap(a)), [a], [c, p])
@@ -165,6 +169,9 @@ def rank_program(g, core, T, topo):
             run("g", lambda e: e.iota(ap(out), pattern, base, mult, allow_small_or_imprecise_dtypes=True), [], [out])
         else:
             run("g", lambda e: e.iota(ap(out), pattern, base, mult), [], [out])
+
+    def pack(a, b):
+        quant(A("wq", a, b), A("wp", a, b), A("wb", 4 * a, 4 * b))
 
     picked, engs = [], {}
     for x in sorted(others, key=lambda x: len(topo.engines(core, T.cores[x]))):
@@ -209,22 +216,24 @@ def rank_program(g, core, T, topo):
 
     iota(A("pcol"), [[0, 1]], 0, 1)
     iota(A("k8"), [[32, 8]], P * r)
-    iota(A("eli", 0, 16), [[ST, 4], [2, 4]], 12)
-    iota(A("eli", 16, 40), [[ST, 4], [1, 3], [3, 2]], 6)
+    iota(A("fri"), [[OWN, 4], [16, ST]], 16)
+    iota(A("eli", 0, 24), [[ST, 4], [1, 3], [3, 2]], 6)
+    iota(A("eli", 24, 88), [[ST, 4], [1, 8], [0, 2]], 12)
+    iota(A("eli", 88, 92), [[ST, 4]], 12)
     iota(A("bli"), [[16, 2], [0, 2]], 0)
     iota(A("lli"), [[8, 2]], 0)
-    iota(A("gli"), [[1, 2], [32, 2]], 0)
-    iota(A("fri"), [[OWN, 4], [16, ST]], 16)
     iota(A("dmi"), [[16, 14]], 385)
-    me = ST * r
-    q8 = 1.0 / 8192
+    iota(A("mxi"), [[16, 24]], PLACES)
+    me, mine = ST * r, (P * r, P * r + P)
     fill(A("land", me + 20, me + 24), 0)
-    for k, (sh, m) in enumerate([(0, 31), (0, 1), (1, 15), (4, 1), (0, 15), (1, 7), (3, 1)]):
+    fill(A("cv", 0, 4 * SLOTS), 0.0)
+    fill(A("zb"), 0.0)
+    for k, (sh, m) in enumerate([(0, 31), (0, 1), (1, 15), (4, 1), (0, 15), (1, 7)]):
         if sh:
             ts(A("pci", k, k + 1), A("pcol"), sh, Op.arith_shift_right, m, Op.bitwise_and)
         else:
             ts(A("pci", k, k + 1), A("pcol"), m, Op.bitwise_and)
-    cp(A("pcf", 0, 7), A("pci", 0, 7))
+    cp(A("pcf", 0, 6), A("pci", 0, 6))
 
     def pf(k):
         return A("pcf", k, k + 1)
@@ -239,23 +248,25 @@ def rank_program(g, core, T, topo):
     ts(pk(6), pf(1), 32.0, Op.mult, pf(5), Op.add)
     tt(pk(2), A("pcf", 8, 9), pk(1), Op.add)
     ts(pk(3), pf(3), 8.0, Op.mult)
-    ts(pk(5), pf(1), 15.0, Op.mult, pf(4), Op.add)
-    ts(A("pkq"), A("pk", 0, 3), q8, Op.mult)
-    fill(A("ein"), 0.0)
-    ts(pk(7), pf(0), 10.0, Op.is_lt)
-    ts(A("lane"), pf(0), 32.0, Op.mult)
-    ts(A("el", 0, 16), A("eli", 0, 16), pf(6), Op.add)
-    cp(A("el", 16, 40), A("eli", 16, 40))
+    ts(pk(4), pf(3), -2.0, Op.mult, 1.0, Op.add)
+    ts(pk(5), pf(3), -1.0, Op.mult, 1.0, Op.add)
+    ts(pk(7), pf(0), 3.0, Op.is_gt)
+    ts(A("lane"), pf(0), 32.0, Op.mult, -128.0, Op.add)
+    cp(A("el", 0, 88), A("eli", 0, 88))
+    ts(A("el", 88, 92), A("eli", 88, 92), pf(5), Op.add)
     ts(A("bl"), A("bli"), pf(4), Op.add)
     ts(A("ll"), A("lli"), pk(6), Op.add)
-    ts(A("gl"), A("gli"), pk(5), Op.add)
-    act(A("fr"), A("fri"), q8)
+    act(A("fr"), A("fri"), 1.0)
     for h in range(4):
         for k, (a, b) in enumerate(((12, 20), (6, 9), (9, 12))):
-            act(A("fr", ST * h + a, ST * h + b), A("fri", ST * h + a, ST * h + b), q8, A("pkq", k, k + 1))
-    act(A("dum"), A("dmi"), 1.0, pf(4))
-    for a in (0, 256, 512, 768):
-        act(A("ex", a, a + 256), A("ein", 0, 256), 0.0)
+            act(A("fr", ST * h + a, ST * h + b), A("fri", ST * h + a, ST * h + b), 1.0, pk(k))
+    for a in (0, 11):
+        cp(A("own14", a, a + 3), A("fr", me + 6, me + 9), "s")
+    gat(A("ex", 1024, 1408), A("fr"), A("el", 0, 24), "s")
+    act(A("ein", 0, 384), A("ex", 1024, 1408), 0.0)
+    act(A("ein", 384, 448), A("ex", 1024, 1088), 0.0)
+    for h in others:
+        gat(A("ex", P * h, P * h + P), A("fr"), A("el", 24 + 16 * h, 40 + 16 * h), "s")
 
     ts(A("xb"), A("xl"), 255, Op.bitwise_and)
     ts(A("xc"), A("xl"), 7, Op.arith_shift_right, 1, Op.bitwise_and)
@@ -278,33 +289,34 @@ def rank_program(g, core, T, topo):
     iota(A("tab", 1024, 2048), [[2, 1024]], 3072)
     iota(A("mv"), [[1, WIN]], 0)
 
-    own = A("fr", me + 12, me + 20)
+    own, zero = A("fr", me + 12, me + 20), float(OWN * r + 1)
     ts(A("ne"), A("xl", 0, 8), 0.0, Op.is_ge)
     ts(A("rk"), A("xl"), 8, Op.arith_shift_right)
-    cp(A("lfo"), A("land", me, me + ST))
     tt(A("z1"), own, A("ne"), Op.mult)
-    ts(A("z2"), A("ne"), -OWN * r * q8, Op.mult, OWN * r * q8, Op.add)
+    ts(A("z2"), A("ne"), -zero, Op.mult, zero, Op.add)
     tt(A("sm"), A("rk", 14, 17), A("rk", 8, 11), Op.is_equal)
     cp(A("rke", 0, 3), A("rk", 8, 11))
+    tt(A("own14", 3, 11), A("z1"), A("z2"), Op.add)
     cp(A("rke", 3, 11), A("rk", 0, 8))
-    tt(own, A("z1"), A("z2"), Op.add)
     ts(A("sm8"), A("sm"), 8.0, Op.mult)
-    tt(A("own14", 0, 3), A("lfo", 6, 9), A("fr", me + 6, me + 9), Op.add)
-    tt(A("own14", 11, 14), A("lfo", 6, 9), A("fr", me + 6, me + 9), Op.add)
     tt(A("rke", 11, 14), A("rk", 14, 17), A("sm8"), Op.subtract)
-    tt(A("own14", 3, 11), A("lfo", 12, 20), own, Op.add)
+    act(A("dum"), A("dmi"), 1.0, pf(4))
+    cp(own, A("own14", 3, 11), "s")
     for j, x in enumerate(others):
         ts(A("msk", 14 * j, 14 * j + 14), A("rke"), float(x), Op.is_equal)
     m3 = [A("msk", 14 * j, 14 * j + 14) for j in range(3)]
     tt(A("any1"), m3[0], m3[1], Op.add)
     for j in range(3):
-        tt(A("ein", 4 * j, 448, 32), m3[j], A("own14"), Op.mult)
+        tt(A("ein", 4 * j + 4, 448, 32), m3[j], A("own14"), Op.mult)
     tt(A("any2"), A("any1"), m3[2], Op.add)
-    fill(A("zb"), 0.0)
-    tt(A("ein", 12, 448, 32), A("any2"), A("own14"), Op.mult)
-    fill(A("cv", 0, 4 * SLOTS), 0.0)
+    tt(A("ein", FLAG, 448, 32), A("any2"), A("own14"), Op.mult)
+    ts(A("mx"), A("mxi"), pf(4), Op.add, pk(5), Op.mult)
     tr(A("dix"), A("ein"))
     run("s", lambda e: e.activation(ap(A("fst")), ap(A("dix")), Act.Sign), [A("dix")], [A("fst")])
+    gat(A("ex", *mine), A("fr"), A("el", 24 + 16 * r, 40 + 16 * r), "s")
+    for j in range(3):
+        act(A("ex", mine[0] + 4 * j + 4, mine[1], 32), A("msk", 14 * j + 3, 14 * j + 11), -2.0, 1.0)
+    act(A("ex", mine[0] + FLAG, mine[1], 32), A("any2", 3, 11), -2.0, 1.0)
     act(A("val"), A("vai"), 1.0, pk(3))
     act(A("d0"), A("lst", 1, 353), 0.0, pk(7))
     quant(A("qo"), A("qop"), A("cv"))
@@ -313,15 +325,13 @@ def rank_program(g, core, T, topo):
     tr(A("oss"), A("scs"))
     tt(A("fo2"), A("dum", 0, 3), A("fo1"), Op.subtract)
     for j in range(3):
-        tt(A("spm", 14 * j, 14 * j + 14), A("oss", 4 * j, 448, 32), m3[j], Op.mult)
+        tt(A("spm", 14 * j, 14 * j + 14), A("oss", 4 * j + 4, 448, 32), m3[j], Op.mult)
     tt(A("b0a"), A("spm", 0, 14), A("spm", 14, 28), Op.add)
     tt(A("b0"), A("b0a"), A("spm", 28, 42), Op.add)
     tt(A("fo3"), A("b0", 0, 3), A("fo2"), Op.add)
     tt(A("b1"), A("b0"), A("dum"), Op.subtract)
     cp(A("fof", 0, 3), A("fo3"))
     sca(A("lst"), A("fof", 0, 3), A("val", 0, 48))
-    quant(A("wq", 0, 512), A("wp", 0, 512), A("wb", 0, 2048))
-    quant(A("wq", 512, 1024), A("wp", 512, 1024), A("wb", 2048, 4096))
     order("y", [A("qo"), A("qop")], [])
     g.sync.dma_start(T.q[:, 0:OWN].bitcast(dt.uint8), T.qo[:, 0:OWN].bitcast(dt.uint8)).then_inc(T.sem.own, 16)
     g.sync.dma_start(T.qp[:, 0:OWN], T.qop[:, 0:OWN]).then_inc(T.sem.own, 16)
@@ -330,51 +340,68 @@ def rank_program(g, core, T, topo):
 
     arrive("arrl", [A("land", ST * x, ST * x + ST) for x in others])
     cp(A("lf"), A("land"))
-    tt(A("dd"), A("lf"), A("fr"), Op.add)
-    gat(A("ex", 512, 1024, 4), A("dd"), A("el", 8, 16), "s")
-    gat(A("ex", 0, 512, 4), A("dd"), A("el", 0, 8))
-    gat(A("ex", 1024, 1408), A("dd"), A("el", 16, 40), "s")
-    tr(A("tab", 0, 512), A("ex", 0, 512))
+    gat(A("ex", 0, 1024, 16), A("lf"), A("el", 88, 92))
     for h in range(4):
         cp(A("to0", 6 * h, 6 * h + 6), A("lf", ST * h, ST * h + 6), "s")
+    for h in range(4):
+        for k in range(2):
+            cp(A("ex", 1024 + 96 * h + 16 * k, 1120 + 96 * h, 32), A("lf", ST * h + 6 + 3 * k, ST * h + 9 + 3 * k), "s")
+    tr(A("tab", 0, 512), A("ex", 0, 512))
+    cp(A("tou"), A("to0"))
     tr(A("tab", 512, 1024), A("ex", 512, 1024))
-    mine = (P * r, P * r + P)
-    first = A("tab", 0, 1024)
-    for h in (2, 3, 0, 1):
-        gat(A("ga0", 96 * h, 96 * h + 96), first, A("land", ST * h, ST * h + 6), "s" if h > 1 else "v")
-    tr(A("ev"), A("ex", 1024, 1408))
-    cp(A("tab", 2048, 3072), A("tab", 1024, 2048), "s")
-    for t in range(3):
-        if t:
-            gat(A("ga%d" % t, 192, 384), A("tab"), A("to%d" % t, 12, 24), "s")
-            gat(A("ga%d" % t, 0, 192), A("tab"), A("to%d" % t, 0, 12))
-            tr(A("gt%d" % t), A("ga%d" % t))
-            sca(A("tab"), A("to%d" % t), A("ga%d" % (t - 1)))
-        else:
-            tr(A("gt0"), A("ga0"))
-            for h in range(4):
-                sca(first, A("land", ST * h, ST * h + 6), A("ev", 96 * h, 96 * h + 96))
-        if t < 2:
-            for h in (2 * t, 2 * t + 1):
-                cp(A("m", OWN * h, OWN * h + OWN), A("mv", 0, OWN), "s")
-        cp(A("sn", P * t, P * t + P), A("tab", *mine), "s")
-        if t:
-            order("y", [A("sn", P * t, P * t + P)], [A("sn", 0, P)])
-            for p in range(8 * t, 128, 32):
-                g.sync.dma_start(T.sn[p:p + 1, 0:P], T.sn[p:p + 1, P * t:P * t + P]).then_inc(T.sem.sns, 16)
-                total["sns"] = total.get("sns", 0) + 16
-        tt(A("ti%d" % (t + 1)), A("gt%d" % t, 0, 384, 16), A("ti%d" % t) if t else A("to0"), Op.subtract)
-        cp(A("to%d" % (t + 1)), A("ti%d" % (t + 1)))
-    note([A("sn", P, 3 * P)], [A("sn", 0, P)], ("sns", total["sns"], {}, "dma"))
+    first, places = A("tab", 0, 1024), A("tab", 0, PLACES)
 
-    tt(A("un", 0, 256), A("tab", *mine), A("dix", 96, 352), Op.is_equal)
+    def spread(t, pairs):
+        order("y", [A("sn", P * t, P * t + P)], [A("sn", 0, P)])
+        for p in range(0, 128, 32):
+            for x, z in pairs:
+                g.sync.dma_start(T.sn[p + z:p + z + 1, 0:P], T.sn[p + x:p + x + 1, P * t:P * t + P]).then_inc(T.sem.sns, 16)
+                total["sns"] = total.get("sns", 0) + 16
+
+    gat(A("ga0", 192, 384), first, A("tou", 12, 24), "s")
+    gat(A("ga0", 0, 192), first, A("tou", 0, 12))
+    cp(A("tab", 2048, 3072), A("tab", 1024, 2048), "s")
+    tr(A("gt0"), A("ga0"))
+    tr(A("ev"), A("ex", 1024, 1408))
+    tt(A("ti1"), A("gt0", 0, 384, 16), A("to0"), Op.subtract)
+    cp(A("to1"), A("ti1"))
+    sca(first, A("tou"), A("ev"))
+    gat(A("ga1", 192, 384), places, A("to1", 12, 24), "s")
+    gat(A("ga1", 0, 192), places, A("to1", 0, 12))
+    cp(A("sn", 0, P), A("tab", *mine), "s")
+    tr(A("gt1"), A("ga1"))
+    tt(A("ti2"), A("gt1", 0, 384, 16), A("ti1"), Op.subtract)
+    cp(A("to2"), A("ti2"))
+    act(A("x2"), A("ti2"), pf(3))
+    act(A("y2"), A("ti2"), pk(4))
+    sca(places, A("to1"), A("ga0"))
+    gat(A("ga2", 256, 384), places, A("to2", 16, 24), "s")
+    tt(A("lcf"), A("x2"), A("mx"), Op.add)
+    gat(A("ga2", 0, 256), places, A("to2", 0, 16))
+    cp(A("lc"), A("lcf"))
+    cp(A("sn", P, 2 * P), A("tab", *mine), "s")
+    gat(A("gc"), A("tab"), A("lc"), "s")
+    tr(A("gt2"), A("ga2"))
+    ts(A("w1"), A("gt2", 0, 384, 16), pf(3), Op.mult)
+    tt(A("ti3"), A("w1"), A("y2"), Op.add)
+    cp(A("to3"), A("ti3"))
+    sca(places, A("to3"), A("gc"))
+    spread(1, ((10, 10), (26, 26)))
+
+    run("s", lambda e: e.activation(ap(A("un", 0, 256)), ap(A("tab", *mine)), Act.Relu, scale=-1.0), [A("tab", *mine)], [A("un", 0, 256)])
     fo = A("land", me, me + 6)
-    run("v", lambda e: e.tensor_tensor(ap(A("un", 256, 352)), ap(first).indirect(ap(fo)), ap(A("dix", 352, 448)), Op.is_equal), [first, fo, A("dix", 352, 448)], [A("un", 256, 352)])
+    run("v", lambda e: e.tensor_tensor(ap(A("un", 256, 352)), ap(first).indirect(ap(fo)), ap(A("dix", 352, 448)), Op.is_equal), [first, fo, A("dix", 352, 448)], [A("un", 256, 352)], True)
+    cp(A("sn", 2 * P, 3 * P), A("tab", *mine), "s")
+    spread(2, ((14, 14), (14, 30), (30, 15), (30, 31)))
+    note([A("sn", P, 3 * P)], [A("sn", 0, P)], ("sns", total["sns"], {}, "dma"))
+    pack(0, 128)
+    for h in range(4):
+        cp(A("m", OWN * h, OWN * h + OWN), A("mv", 0, OWN), "s")
     scan(A("sc"), A("d0"), A("un"), 0.0, Op.mult, Op.add)
     tr(A("osd"), A("sc"))
     for j in range(3):
-        tt(A("cm", 11 * j, 11 * j + 11), A("osd", 4 * j, 352, 32), A("msk", 14 * j + 3, 14 * j + 14), Op.mult)
-    tt(A("fl"), A("any2", 3, 14), A("osd", 12, 352, 32), Op.subtract)
+        tt(A("cm", 11 * j, 11 * j + 11), A("osd", 4 * j + 4, 352, 32), A("msk", 14 * j + 3, 14 * j + 14), Op.mult)
+    tt(A("fl"), A("any2", 3, 14), A("osd", FLAG, 352, 32), Op.subtract)
     tt(A("cs1"), A("cm", 0, 11), A("cm", 11, 22), Op.add)
     tt(A("bb"), A("b1", 3, 14), A("cm", 22, 33), Op.subtract)
     tt(A("cs2"), A("bb"), A("cs1"), Op.subtract)
@@ -398,27 +425,34 @@ def rank_program(g, core, T, topo):
     post("arrq", "lsq", [A("sq%d" % j) for j in range(3)], [A("q", *x) for x in land])
     post("arrp", "lsp", [A("sqp%d" % j) for j in range(3)], [A("qp", *x) for x in land])
 
-    sca(A("tab"), A("to3"), A("ga2"))
-    tr(A("ts", 0, 256), A("sn", 0, 256))
-    tr(A("ts", 256, 512), A("tab", *mine))
-    cp(A("idi", 0, 32), A("ts", 0, 256, 8))
-    cp(A("idi", 32, 40), A("ts", 256, 512, 32))
-    tt(A("idf", 0, 32), A("ts", 0, 256, 8), A("idi", 0, 32), Op.subtract)
-    tt(A("idf", 32, 40), A("ts", 256, 512, 32), A("idi", 32, 40), Op.subtract)
-    ts(A("ido"), A("idf", 0, 32), 8192.0, Op.mult)
-    ts(A("ido", 3, 32, 4), A("idf", 32, 40), 8192.0, Op.mult)
+    tr(A("ts"), A("sn", 0, 256))
+    now = [A("ts", x, 256, 16) for x in (6, 10, 14, 15)]
+    tt(A("ne3"), now[3], now[1], Op.not_equal)
+    tt(A("df3"), now[3], now[2], Op.subtract)
+    cp(A("ido", 0, 16), now[0])
+    tt(A("pr3"), A("ne3"), A("df3"), Op.mult)
+    cp(A("ido", 16, 32), now[1])
+    tt(A("r3"), A("pr3"), now[2], Op.add)
+    cp(A("ido", 32, 48), now[2])
+    cp(A("ido", 48, 64), A("r3"))
+    pack(128, 640)
+    pack(640, 1024)
     arrive("arrm", [A("lin", 8 * k, 8 * k + 8) for k in range(3)])
     for k, x in enumerate(others):
         sca(A("m", OWN * x, OWN * x + OWN), A("lin", 8 * k, 8 * k + 7), A("mv", OWN + SLOTS * k, OWN + SLOTS * k + SLOTS))
-    gat(A("mg", 256, 512), A("m"), A("ido", 16, 32), "s")
-    gat(A("mg", 0, 256), A("m"), A("ido", 0, 16))
-    tr(A("om"), A("mg"))
-    cp(A("yb", 0, 16), A("om", 0, 512, 32))
-    cp(A("yb", 16, 32), A("om", 16, 512, 32))
-    tr(A("yt"), A("yb"))
-    gat(A("yg"), A("yt"), A("bl"))
-    tr(A("yh"), A("yg"))
-    gat(A("off"), A("yh"), A("gl"))
+
+    def look(t):
+        a = P * t
+        if t:
+            gat(A("mg", a, a + P), A("m"), A("ido", 16 * t, 16 * t + 16), "s")
+        else:
+            gat(A("mg", 128, 256), A("m"), A("ido", 8, 16), "s")
+            gat(A("mg", 0, 128), A("m"), A("ido", 0, 8))
+
+    def turn(t):
+        a = P * t
+        tr(A("om", a, a + P), A("mg", a, a + P))
+        cp(A("off", 16 * t, 16 * t + 16), A("om", a, a + P, 16))
 
     arrive("arrq", [A("q", OWN, WIN)])
     arrive("arrp", [A("qp", OWN, WIN)])
@@ -435,16 +469,27 @@ def rank_program(g, core, T, topo):
         for o in range(O):
             i = O * t + o
             for b in range(2):
-                cp(A("ys", P * i + 128 * b, P * i + 128 * b + 128), A("ps", 512 * i + b, 512 * i + P, 2), "vs"[o])
+                cp(A("ys", P * i + 128 * b, P * i + 128 * b + 128), A("ps", 512 * i + b, 512 * i + P, 2), "s" if t < 1 else "vs"[o])
             reg = A("ys", P * i, P * i + P)
             order("y", [reg], [])
             g.sync.dma_start(T.y[:, P * i:P * i + P], ap(reg)).then_inc(T.sem.sty, 16)
             total["sty"] = total.get("sty", 0) + 16
-    for t in range(R):
-        table(t)
-        if t:
-            out(t - 1)
-    out(R - 1)
+    look(0)
+    look(1)
+    look(2)
+    turn(0)
+    turn(1)
+    table(0)
+    look(3)
+    turn(2)
+    table(1)
+    turn(3)
+    out(0)
+    table(2)
+    out(1)
+    table(3)
+    out(2)
+    out(3)
     for q in ("v", "s", "t", "g"):
         total[sem_of[q]] = cnt[sem_of[q]]
     for s in SEMAPHORES:

from concourse.bass import DstId, RemoteDMATransfer
from concourse.mybir import dt, AluOpType as Op, ActivationFunctionType as Act

N, P, V, R, O = 4, 256, 96, 4, 2
SLOTS = 112
OWN = SLOTS + V + P
WIN = OWN + 3 * SLOTS
ST = 24
FLAG = 2
PLACES = 3072
F32, I32, U16, BF, CODE, PL = "float32", "int32", "uint16", "bfloat16", "float8_e4m3fn_x4", "uint8"


def _s(n, t):
    return ("sbuf", [128, n], t)


SCRATCH = {
    "xl": _s(20, I32), "pcol": _s(1, I32), "pci": _s(7, I32), "pcf": _s(9, F32), "pk": _s(8, F32), "lane": _s(1, F32),
    "k8": _s(8, F32), "pos": _s(8, F32), "ke": _s(8, F32), "xi": _s(120, I32), "xf": _s(48, F32), "ss": _s(14, F32),
    "land": _s(4 * ST, U16), "dd": _s(8 * ST, F32), "fri": _s(4 * ST, F32),
    "eli": _s(92, F32), "el": _s(92, U16), "ex": _s(1408, F32), "tab": _s(PLACES + 384, F32), "ev": _s(384, F32), "to0": _s(24, F32), "tou": _s(24, U16),
    "gc": _s(384, F32), "mxi": _s(24, F32), "mx": _s(24, F32), "x2": _s(24, F32), "y2": _s(24, F32), "lcf": _s(24, F32), "lc": _s(24, U16), "w1": _s(24, F32),
    "ne3": _s(16, F32), "df3": _s(16, F32), "pr3": _s(16, F32), "r3": _s(16, F32),
    "dmi": _s(14, F32), "dum": _s(14, F32), "vai": _s(224, F32), "val": _s(224, F32),
    "bli": _s(4, F32), "bl": _s(4, U16), "lli": _s(2, F32), "ll": _s(2, U16),
    "rke": _s(14, F32), "sm": _s(3, F32), "sm8": _s(3, F32), "own14": _s(14, F32), "msk": _s(42, F32), "any1": _s(14, F32), "any2": _s(14, F32),
    "ein": _s(448, F32), "dix": _s(448, F32), "fst": _s(448, F32), "scs": _s(448, F32), "d0": _s(352, F32),
    "oss": _s(448, F32), "spm": _s(42, F32), "b0a": _s(14, F32), "b0": _s(14, F32), "b1": _s(14, F32),
    "fo1": _s(3, F32), "fo2": _s(3, F32), "fo3": _s(3, F32), "fof": _s(4, U16), "lst": _s(616, F32),
    "un": _s(352, F32), "sc": _s(352, F32), "osd": _s(352, F32), "cm": _s(33, F32), "cs1": _s(11, F32), "cs2": _s(11, F32),
    "fl": _s(11, F32), "bb": _s(11, F32), "fb": _s(11, F32), "of1": _s(11, F32), "ofd": _s(12, U16),
    "olt": _s(384, F32), "zb": _s(32, F32), "zt": _s(32, F32), "zg": _s(64, F32), "zh": _s(64, F32), "loff": _s(32, U16),
    "lin": _s(24, U16), "mv": _s(WIN, F32), "m": _s(4 * OWN, F32),
    "sn": _s(768, F32), "ts": _s(256, F32), "ido": _s(64, U16), "mg": _s(1024, F32), "om": _s(1024, F32), "off": _s(64, U16),
    "cv": _s(4 * OWN, BF), "qo": _s(OWN, CODE), "qop": _s(OWN, PL), "q": _s(WIN, CODE), "qp": _s(WIN, PL),
    "wb": _s(4096, BF), "wq": _s(1024, CODE), "wp": _s(1024, PL), "ys": _s(2048, F32),
    "ga0": _s(384, F32), "ga2": _s(384, F32),
    "ps": ("psum", [128, 4096], F32),
}
for _t in range(3):
    SCRATCH["gt%d" % _t] = _s(384, F32)
    SCRATCH["ti%d" % (_t + 1)] = _s(24, F32)
    SCRATCH["to%d" % (_t + 1)] = _s(24, U16)
    SCRATCH["sq%d" % _t] = _s(SLOTS, CODE)
    SCRATCH["sqp%d" % _t] = _s(SLOTS, PL)
for _t in range(4):
    SCRATCH["k%d" % _t] = _s(P, CODE)
    SCRATCH["kp%d" % _t] = _s(P, PL)
PART = {n: ("xi", 20 * k, 20) for k, n in enumerate(["xb", "xc", "xd", "xt", "xp", "rk"])}
PART.update({n: ("xf", 8 * k, 8) for k, n in enumerate(["emp", "p1", "we", "ne", "z1", "z2"])})
PART.update({"ga1": ("tab", PLACES, 384), "lf": ("dd", 0, 4 * ST), "fr": ("dd", 4 * ST, 4 * ST)})

SEMAPHORES = ["sv", "ss", "st", "sg", "ldx", "ldv", "ldc", "ldw0", "ldw1", "arrl", "arrm", "arrq", "arrp", "lsl", "lsm", "lsq", "lsp", "sty", "own", "sns"]


def rank_program(g, core, T, topo):
    r = T.rank_of(core)
    if r is None:
        return
    others = [x for x in range(N) if x != r]
    eng = {"v": g.vector, "s": g.scalar, "t": g.tensor, "g": g, "y": g.sync}
    sem_of = {"v": "sv", "s": "ss", "t": "st", "g": "sg"}
    cnt, known, log, total = {}, {k: {} for k in eng}, {}, {}

    def clash(a, b):
        if a[0] >= b[1] or b[0] >= a[1]:
            return False
        return not (a[2] == b[2] and a[2] > 1 and (a[0] - b[0]) % a[2])

    def wait(q, tok):
        s, v, clock, _ = tok
        if known[q].get(s, 0) >= v:
            return
        eng[q].wait_ge(T.sem[s], v)
        for k, x in list(clock.items()) + [(s, v)]:
            known[q][k] = max(known[q].get(k, 0), x)

    def order(q, reads, writes):
        need = []
        for regs, w in ((reads, False), (writes, True)):
            for n, lo, hi, st in regs:
                for l2, h2, s2, w2, tok in log.get(n, []):
                    if not (w or w2) or not clash((lo, hi, st), (l2, h2, s2)):
                        continue
                    if w and not w2 and tok[3] == q:
                        continue
                    need.append(tok)
        for tok in sorted(need, key=lambda t: -t[1]):
            wait(q, tok)

    def note(reads, writes, tok):
        for regs, w in ((reads, False), (writes, True)):
            for n, lo, hi, st in regs:
                log.setdefault(n, []).append((lo, hi, st, w, tok))

    def run(q, call, reads, writes, listed=False):
        order(q, reads, writes)
        s = sem_of[q]
        cnt[s] = cnt.get(s, 0) + 1
        call(eng[q]).then_inc(T.sem[s], 1)
        note(reads, writes, (s, cnt[s], dict(known[q]), "list" if listed else q))

    def load(q, sem, tot, out, in_, region):
        eng[q].dma_start(out, in_).then_inc(T.sem[sem], 16)
        total[sem] = tot
        note([], [region], (sem, tot, {}, "dma"))

    def ap(x):
        n, lo, hi, st = x
        return T[n][:, lo:hi] if st == 1 else T[n][:, lo:hi:st]

    def A(n, lo=0, hi=None, st=1):
        if n in PART:
            b, o, w = PART[n]
            return (b, o + lo, o + (w if hi is None else hi), st)
        return (n, lo, SCRATCH[n][1][1] if hi is None else hi, st)

    def sc_(x):
        return ap(x) if isinstance(x, tuple) else x

    def aps(*xs):
        return [x for x in xs if isinstance(x, tuple)]

    def tt(out, a, b, op):
        run("v", lambda e: e.tensor_tensor(ap(out), ap(a), ap(b), op), [a, b], [out])

    def ts(out, a, s1, op, s2=None, op1=None):
        if op1 is None:
            run("v", lambda e: e.tensor_scalar(ap(out), ap(a), sc_(s1), None, op), [a] + aps(s1), [out])
        else:
            run("v", lambda e: e.tensor_scalar(ap(out), ap(a), sc_(s1), sc_(s2), op, op1), [a] + aps(s1, s2), [out])

    def cp(out, a, q="v"):
        if q == "v":
            run("v", lambda e: e.tensor_copy(ap(out), ap(a)), [a], [out])
        else:
            run("s", lambda e: e.activation(ap(out), ap(a), Act.Copy), [a], [out])

    def act(out, a, scale, bias=0.0):
        run("s", lambda e: e.activation(ap(out), ap(a), Act.Identity, bias=sc_(bias), scale=sc_(scale)), [a] + aps(scale, bias), [out])

    def tr(out, a):
        run("v", lambda e: e.transpose(ap(out), ap(a)), [a], [out])

    def scan(out, a, b, start, op0, op1):
        run("v", lambda e: e.tensor_tensor_scan(ap(out), ap(a), ap(b), sc_(start), op0, op1), [a, b] + aps(start), [out])

    def fill(out, c):
        run("v", lambda e: e.memset(ap(out), c), [], [out])

    def gat(out, win, off, q="v"):
        if q == "v":
            run("v", lambda e: e.tensor_copy(ap(out), ap(win).indirect(ap(off))), [win, off], [out], True)
        else:
            run("s", lambda e: e.activation(ap(out), ap(win).indirect(ap(off)), Act.Copy), [win, off], [out], True)

    def sca(win, off, a):
        run("v", lambda e: e.tensor_copy(ap(win).indirect(ap(off)), ap(a)), [off, a], [win])

    def pick(out, win, off):
        run("v", lambda e: e.tensor_copy(ap(out).bitcast(dt.uint32), ap(win).bitcast(dt.uint32).indirect(ap(off))), [win, off], [out], True)

    def quant(c, p, a):
        run("v", lambda e: e.quantize_mx(ap(c), ap(p), ap(a)), [a], [c, p])

    def iota(out, pattern, base, mult=0):
        if SCRATCH[out[0]][2] == F32:
            run("g", lambda e: e.iota(ap(out), pattern, base, mult, allow_small_or_imprecise_dtypes=True), [], [out])
        else:
            run("g", lambda e: e.iota(ap(out), pattern, base, mult), [], [out])

    def pack(a, b):
        quant(A("wq", a, b), A("wp", a, b), A("wb", 4 * a, 4 * b))

    picked, engs = [], {}
    for x in sorted(others, key=lambda x: len(topo.engines(core, T.cores[x]))):
        e = [k for k in topo.engines(core, T.cores[x]) if k not in picked][:4]
        picked += e
        engs[x] = e

    def post(sem, lsem, srcs, dsts):
        order("g", srcs, [])
        trs = []
        for j, x in enumerate(others):
            rid, pid, _ = topo.addr(T.cores[x])
            s, d = ap(srcs[j]), ap(dsts[j])
            if SCRATCH[srcs[j][0]][2] == CODE:
                s, d = s.bitcast(dt.uint8), d.bitcast(dt.uint8)
            trs.append(RemoteDMATransfer(dst_ids=[DstId(rid=rid, pnc=pid)], dma_engine_mask=sum(1 << k for k in engs[x]), remote_sem=T.sem[sem], src=s, dst=d))
        g.remote_dma_fused(trs, local_sem=T.sem[lsem])
        total[lsem] = sum(len(engs[x]) for x in others)

    def arrive(sem, regions):
        total[sem] = 4 * len(others)
        note([], regions, (sem, 4 * len(others), {}, "far"))

    jobs = []
    for b in range(4):
        jobs.append((T.xl[32 * b:32 * b + 32, 8:11], T.f1[:, :]))
        jobs.append((T.xl[32 * b:32 * b + 32, 14:17], T.f2[:, :]))
        jobs.append((T.xl[32 * b:32 * b + 32, 0:8], T.alt[:, :]))
    for n, c in ((T.f1, 11), (T.f2, 17)):
        for b in range(3):
            jobs.append((T.xl[32 * b + 16:32 * b + 48, c:c + 3], n[:, :]))
        jobs.append((T.xl[0:16, c:c + 3], n[8:16, :]))
        jobs.append((T.xl[112:128, c:c + 3], n[0:8, :]))
    for k, (o, i) in enumerate(jobs):
        eng["ys"[k % 2]].dma_start(o, i).then_inc(T.sem.ldx, 16)
    total["ldx"] = 16 * len(jobs)
    note([], [A("xl")], ("ldx", 16 * len(jobs), {}, "dma"))
    load("y", "ldv", 16, T.cv[:, 4 * SLOTS:4 * SLOTS + 4 * V], T.v[:, :], A("cv", 4 * SLOTS, 4 * SLOTS + 4 * V))
    load("y", "ldc", 16, T.cv[:, 4 * SLOTS + 4 * V:4 * OWN], T.c[:, :], A("cv", 4 * SLOTS + 4 * V, 4 * OWN))
    for k in range(2):
        load("y", "ldw%d" % k, 16, T.wb[:, 2048 * k:2048 * k + 2048], T.w[:, 2048 * k:2048 * k + 2048], A("wb", 2048 * k, 2048 * k + 2048))

    iota(A("pcol"), [[0, 1]], 0, 1)
    iota(A("k8"), [[32, 8]], P * r)
    iota(A("fri"), [[OWN, 4], [16, ST]], 16)
    iota(A("eli", 0, 24), [[ST, 4], [1, 3], [3, 2]], 6)
    iota(A("eli", 24, 88), [[ST, 4], [1, 8], [0, 2]], 12)
    iota(A("eli", 88, 92), [[ST, 4]], 12)
    iota(A("bli"), [[16, 2], [0, 2]], 0)
    iota(A("lli"), [[8, 2]], 0)
    iota(A("dmi"), [[16, 14]], 385)
    iota(A("mxi"), [[16, 24]], PLACES)
    me, mine = ST * r, (P * r, P * r + P)
    fill(A("land", me + 20, me + 24), 0)
    fill(A("cv", 0, 4 * SLOTS), 0.0)
    fill(A("zb"), 0.0)
    for k, (sh, m) in enumerate([(0, 31), (0, 1), (1, 15), (4, 1), (0, 15), (1, 7)]):
        if sh:
            ts(A("pci", k, k + 1), A("pcol"), sh, Op.arith_shift_right, m, Op.bitwise_and)
        else:
            ts(A("pci", k, k + 1), A("pcol"), m, Op.bitwise_and)
    cp(A("pcf", 0, 6), A("pci", 0, 6))

    def pf(k):
        return A("pcf", k, k + 1)

    def pk(k):
        return A("pk", k, k + 1)
    ts(A("pos"), A("k8"), pf(0), Op.add)
    ts(A("ke"), A("k8"), pf(0), Op.add, 1025.0, Op.add)
    ts(pk(0), pf(1), 128.0, Op.mult, pf(2), Op.add)
    ts(pk(1), pf(1), 48.0, Op.mult, pf(2), Op.add)
    ts(A("pcf", 8, 9), pf(3), -16.0, Op.mult, -40.0, Op.add)
    ts(pk(6), pf(1), 32.0, Op.mult, pf(5), Op.add)
    tt(pk(2), A("pcf", 8, 9), pk(1), Op.add)
    ts(pk(3), pf(3), 8.0, Op.mult)
    ts(pk(4), pf(3), -2.0, Op.mult, 1.0, Op.add)
    ts(pk(5), pf(3), -1.0, Op.mult, 1.0, Op.add)
    ts(pk(7), pf(0), 3.0, Op.is_gt)
    ts(A("lane"), pf(0), 32.0, Op.mult, -128.0, Op.add)
    cp(A("el", 0, 88), A("eli", 0, 88))
    ts(A("el", 88, 92), A("eli", 88, 92), pf(5), Op.add)
    ts(A("bl"), A("bli"), pf(4), Op.add)
    ts(A("ll"), A("lli"), pk(6), Op.add)
    act(A("fr"), A("fri"), 1.0)
    for h in range(4):
        for k, (a, b) in enumerate(((12, 20), (6, 9), (9, 12))):
            act(A("fr", ST * h + a, ST * h + b), A("fri", ST * h + a, ST * h + b), 1.0, pk(k))
    for a in (0, 11):
        cp(A("own14", a, a + 3), A("fr", me + 6, me + 9), "s")
    gat(A("ex", 1024, 1408), A("fr"), A("el", 0, 24), "s")
    act(A("ein", 0, 384), A("ex", 1024, 1408), 0.0)
    act(A("ein", 384, 448), A("ex", 1024, 1088), 0.0)
    for h in others:
        gat(A("ex", P * h, P * h + P), A("fr"), A("el", 24 + 16 * h, 40 + 16 * h), "s")

    ts(A("xb"), A("xl"), 255, Op.bitwise_and)
    ts(A("xc"), A("xl"), 7, Op.arith_shift_right, 1, Op.bitwise_and)
    ts(A("emp"), A("xl", 0, 8), 0.0, Op.is_lt)
    ts(A("xd"), A("xc"), -255.0, Op.mult)
    tt(A("xt"), A("xl"), A("xb"), Op.add)
    tt(A("we"), A("emp"), A("ke"), Op.mult)
    tt(A("xp"), A("xt"), A("xd"), Op.add)
    tt(A("p1"), A("we"), A("pos"), Op.add)
    cp(A("land", me, me + 6, 2), A("xp", 8, 11))
    cp(A("land", me + 1, me + 6, 2), A("xp", 11, 14))
    tt(A("ss", 0, 6), A("xp", 8, 14), A("xp", 14, 20), Op.add)
    tt(A("ss", 6, 14), A("xp", 0, 8), A("p1"), Op.add)
    cp(A("land", me + 6, me + 20), A("ss"))
    post("arrl", "lsl", [A("land", me, me + ST)] * 3, [A("land", me, me + ST)] * 3)
    iota(A("vai", 0, 48), [[16, 3], [1, 8], [48, 2]], SLOTS)
    iota(A("vai", 48, 176), [[16, 8], [1, 8], [128, 2]], SLOTS + V)
    iota(A("vai", 176, 224), [[16, 3], [1, 8], [48, 2]], SLOTS)
    iota(A("lst", 1, 385), [[0, 3], [1, 128]], 0)
    iota(A("tab", 1024, 2048), [[2, 1024]], 3072)
    iota(A("mv"), [[1, WIN]], 0)

    own, zero = A("fr", me + 12, me + 20), float(OWN * r + 1)
    ts(A("ne"), A("xl", 0, 8), 0.0, Op.is_ge)
    ts(A("rk"), A("xl"), 8, Op.arith_shift_right)
    tt(A("z1"), own, A("ne"), Op.mult)
    ts(A("z2"), A("ne"), -zero, Op.mult, zero, Op.add)
    tt(A("sm"), A("rk", 14, 17), A("rk", 8, 11), Op.is_equal)
    cp(A("rke", 0, 3), A("rk", 8, 11))
    tt(A("own14", 3, 11), A("z1"), A("z2"), Op.add)
    cp(A("rke", 3, 11), A("rk", 0, 8))
    ts(A("sm8"), A("sm"), 8.0, Op.mult)
    tt(A("rke", 11, 14), A("rk", 14, 17), A("sm8"), Op.subtract)
    act(A("dum"), A("dmi"), 1.0, pf(4))
    cp(own, A("own14", 3, 11), "s")
    for j, x in enumerate(others):
        ts(A("msk", 14 * j, 14 * j + 14), A("rke"), float(x), Op.is_equal)
    m3 = [A("msk", 14 * j, 14 * j + 14) for j in range(3)]
    tt(A("any1"), m3[0], m3[1], Op.add)
    for j in range(3):
        tt(A("ein", 4 * j + 4, 448, 32), m3[j], A("own14"), Op.mult)
    tt(A("any2"), A("any1"), m3[2], Op.add)
    tt(A("ein", FLAG, 448, 32), A("any2"), A("own14"), Op.mult)
    ts(A("mx"), A("mxi"), pf(4), Op.add, pk(5), Op.mult)
    tr(A("dix"), A("ein"))
    run("s", lambda e: e.activation(ap(A("fst")), ap(A("dix")), Act.Sign), [A("dix")], [A("fst")])
    gat(A("ex", *mine), A("fr"), A("el", 24 + 16 * r, 40 + 16 * r), "s")
    for j in range(3):
        act(A("ex", mine[0] + 4 * j + 4, mine[1], 32), A("msk", 14 * j + 3, 14 * j + 11), -2.0, 1.0)
    act(A("ex", mine[0] + FLAG, mine[1], 32), A("any2", 3, 11), -2.0, 1.0)
    act(A("val"), A("vai"), 1.0, pk(3))
    act(A("d0"), A("lst", 1, 353), 0.0, pk(7))
    quant(A("qo"), A("qop"), A("cv"))
    tt(A("fo1"), A("any2", 0, 3), A("dum", 0, 3), Op.mult)
    scan(A("scs"), A("fst"), A("fst"), A("lane"), Op.add, Op.max)
    tr(A("oss"), A("scs"))
    tt(A("fo2"), A("dum", 0, 3), A("fo1"), Op.subtract)
    for j in range(3):
        tt(A("spm", 14 * j, 14 * j + 14), A("oss", 4 * j + 4, 448, 32), m3[j], Op.mult)
    tt(A("b0a"), A("spm", 0, 14), A("spm", 14, 28), Op.add)
    tt(A("b0"), A("b0a"), A("spm", 28, 42), Op.add)
    tt(A("fo3"), A("b0", 0, 3), A("fo2"), Op.add)
    tt(A("b1"), A("b0"), A("dum"), Op.subtract)
    cp(A("fof", 0, 3), A("fo3"))
    sca(A("lst"), A("fof", 0, 3), A("val", 0, 48))
    order("y", [A("qo"), A("qop")], [])
    g.sync.dma_start(T.q[:, 0:OWN].bitcast(dt.uint8), T.qo[:, 0:OWN].bitcast(dt.uint8)).then_inc(T.sem.own, 16)
    g.sync.dma_start(T.qp[:, 0:OWN], T.qop[:, 0:OWN]).then_inc(T.sem.own, 16)
    total["own"] = 32
    note([], [A("q", 0, OWN), A("qp", 0, OWN)], ("own", 32, {}, "dma"))

    arrive("arrl", [A("land", ST * x, ST * x + ST) for x in others])
    cp(A("lf"), A("land"))
    gat(A("ex", 0, 1024, 16), A("lf"), A("el", 88, 92))
    for h in range(4):
        cp(A("to0", 6 * h, 6 * h + 6), A("lf", ST * h, ST * h + 6), "s")
    for h in range(4):
        for k in range(2):
            cp(A("ex", 1024 + 96 * h + 16 * k, 1120 + 96 * h, 32), A("lf", ST * h + 6 + 3 * k, ST * h + 9 + 3 * k), "s")
    tr(A("tab", 0, 512), A("ex", 0, 512))
    cp(A("tou"), A("to0"))
    tr(A("tab", 512, 1024), A("ex", 512, 1024))
    first, places = A("tab", 0, 1024), A("tab", 0, PLACES)

    def spread(t, pairs):
        order("y", [A("sn", P * t, P * t + P)], [A("sn", 0, P)])
        for p in range(0, 128, 32):
            for x, z in pairs:
                g.sync.dma_start(T.sn[p + z:p + z + 1, 0:P], T.sn[p + x:p + x + 1, P * t:P * t + P]).then_inc(T.sem.sns, 16)
                total["sns"] = total.get("sns", 0) + 16

    gat(A("ga0", 192, 384), first, A("tou", 12, 24), "s")
    gat(A("ga0", 0, 192), first, A("tou", 0, 12))
    cp(A("tab", 2048, 3072), A("tab", 1024, 2048), "s")
    tr(A("gt0"), A("ga0"))
    tr(A("ev"), A("ex", 1024, 1408))
    tt(A("ti1"), A("gt0", 0, 384, 16), A("to0"), Op.subtract)
    cp(A("to1"), A("ti1"))
    sca(first, A("tou"), A("ev"))
    gat(A("ga1", 192, 384), places, A("to1", 12, 24), "s")
    gat(A("ga1", 0, 192), places, A("to1", 0, 12))
    cp(A("sn", 0, P), A("tab", *mine), "s")
    tr(A("gt1"), A("ga1"))
    tt(A("ti2"), A("gt1", 0, 384, 16), A("ti1"), Op.subtract)
    cp(A("to2"), A("ti2"))
    act(A("x2"), A("ti2"), pf(3))
    act(A("y2"), A("ti2"), pk(4))
    sca(places, A("to1"), A("ga0"))
    gat(A("ga2", 256, 384), places, A("to2", 16, 24), "s")
    tt(A("lcf"), A("x2"), A("mx"), Op.add)
    gat(A("ga2", 0, 256), places, A("to2", 0, 16))
    cp(A("lc"), A("lcf"))
    cp(A("sn", P, 2 * P), A("tab", *mine), "s")
    gat(A("gc"), A("tab"), A("lc"), "s")
    tr(A("gt2"), A("ga2"))
    ts(A("w1"), A("gt2", 0, 384, 16), pf(3), Op.mult)
    tt(A("ti3"), A("w1"), A("y2"), Op.add)
    cp(A("to3"), A("ti3"))
    sca(places, A("to3"), A("gc"))
    spread(1, ((10, 10), (26, 26)))

    run("s", lambda e: e.activation(ap(A("un", 0, 256)), ap(A("tab", *mine)), Act.Relu, scale=-1.0), [A("tab", *mine)], [A("un", 0, 256)])
    fo = A("land", me, me + 6)
    run("v", lambda e: e.tensor_tensor(ap(A("un", 256, 352)), ap(first).indirect(ap(fo)), ap(A("dix", 352, 448)), Op.is_equal), [first, fo, A("dix", 352, 448)], [A("un", 256, 352)], True)
    cp(A("sn", 2 * P, 3 * P), A("tab", *mine), "s")
    spread(2, ((14, 14), (14, 30), (30, 15), (30, 31)))
    note([A("sn", P, 3 * P)], [A("sn", 0, P)], ("sns", total["sns"], {}, "dma"))
    pack(0, 128)
    for h in range(4):
        cp(A("m", OWN * h, OWN * h + OWN), A("mv", 0, OWN), "s")
    scan(A("sc"), A("d0"), A("un"), 0.0, Op.mult, Op.add)
    tr(A("osd"), A("sc"))
    for j in range(3):
        tt(A("cm", 11 * j, 11 * j + 11), A("osd", 4 * j + 4, 352, 32), A("msk", 14 * j + 3, 14 * j + 14), Op.mult)
    tt(A("fl"), A("any2", 3, 14), A("osd", FLAG, 352, 32), Op.subtract)
    tt(A("cs1"), A("cm", 0, 11), A("cm", 11, 22), Op.add)
    tt(A("bb"), A("b1", 3, 14), A("cm", 22, 33), Op.subtract)
    tt(A("cs2"), A("bb"), A("cs1"), Op.subtract)
    tt(A("fb"), A("fl"), A("cs2"), Op.mult)
    tt(A("of1"), A("fb"), A("dum", 3, 14), Op.add)
    cp(A("ofd", 0, 11), A("of1"))
    sca(A("lst"), A("ofd", 0, 11), A("val", 48, 224))
    tr(A("olt"), A("lst", 1, 385))
    tt(A("zb", 0, 12), A("olt", 0, 384, 32), A("olt", 16, 384, 32), Op.max)
    tr(A("zt"), A("zb"))
    gat(A("zg"), A("zt"), A("bl"))
    tr(A("zh"), A("zg"))
    gat(A("loff"), A("zh"), A("ll"))
    lists = [A("loff", 8 * j, 8 * j + 7) for j in range(3)]
    at = [sorted(y for y in range(N) if y != x).index(r) for x in others]
    post("arrm", "lsm", [A("loff", 8 * j, 8 * j + 8) for j in range(3)], [A("lin", 8 * k, 8 * k + 8) for k in at])
    for j in range(3):
        pick(A("sq%d" % j), A("qo"), lists[j])
        gat(A("sqp%d" % j), A("qop"), lists[j], "s")
    land = [(OWN + SLOTS * k, OWN + SLOTS * k + SLOTS) for k in at]
    post("arrq", "lsq", [A("sq%d" % j) for j in range(3)], [A("q", *x) for x in land])
    post("arrp", "lsp", [A("sqp%d" % j) for j in range(3)], [A("qp", *x) for x in land])

    tr(A("ts"), A("sn", 0, 256))
    now = [A("ts", x, 256, 16) for x in (6, 10, 14, 15)]
    tt(A("ne3"), now[3], now[1], Op.not_equal)
    tt(A("df3"), now[3], now[2], Op.subtract)
    cp(A("ido", 0, 16), now[0])
    tt(A("pr3"), A("ne3"), A("df3"), Op.mult)
    cp(A("ido", 16, 32), now[1])
    tt(A("r3"), A("pr3"), now[2], Op.add)
    cp(A("ido", 32, 48), now[2])
    cp(A("ido", 48, 64), A("r3"))
    pack(128, 640)
    pack(640, 1024)
    arrive("arrm", [A("lin", 8 * k, 8 * k + 8) for k in range(3)])
    for k, x in enumerate(others):
        sca(A("m", OWN * x, OWN * x + OWN), A("lin", 8 * k, 8 * k + 7), A("mv", OWN + SLOTS * k, OWN + SLOTS * k + SLOTS))

    def look(t):
        a = P * t
        if t:
            gat(A("mg", a, a + P), A("m"), A("ido", 16 * t, 16 * t + 16), "s")
        else:
            gat(A("mg", 128, 256), A("m"), A("ido", 8, 16), "s")
            gat(A("mg", 0, 128), A("m"), A("ido", 0, 8))

    def turn(t):
        a = P * t
        tr(A("om", a, a + P), A("mg", a, a + P))
        cp(A("off", 16 * t, 16 * t + 16), A("om", a, a + P, 16))

    arrive("arrq", [A("q", OWN, WIN)])
    arrive("arrp", [A("qp", OWN, WIN)])

    def table(t):
        pick(A("k%d" % t), A("q"), A("off", 16 * t, 16 * t + 16))
        gat(A("kp%d" % t), A("qp"), A("off", 16 * t, 16 * t + 16), "s")
        for o in range(O):
            i = O * t + o
            wq, wp, kq, kp, z = A("wq", 128 * i, 128 * i + 128), A("wp", 128 * i, 128 * i + 128), A("k%d" % t), A("kp%d" % t), A("ps", 512 * i, 512 * i + P)
            run("t", lambda e: e.matmul_mx(ap(z), ap(wq), ap(wp), ap(kq), ap(kp), True, True), [wq, wp, kq, kp], [z])

    def out(t):
        for o in range(O):
            i = O * t + o
            for b in range(2):
                cp(A("ys", P * i + 128 * b, P * i + 128 * b + 128), A("ps", 512 * i + b, 512 * i + P, 2), "s" if t < 1 else "vs"[o])
            reg = A("ys", P * i, P * i + P)
            order("y", [reg], [])
            g.sync.dma_start(T.y[:, P * i:P * i + P], ap(reg)).then_inc(T.sem.sty, 16)
            total["sty"] = total.get("sty", 0) + 16
    look(0)
    look(1)
    look(2)
    turn(0)
    turn(1)
    table(0)
    look(3)
    turn(2)
    table(1)
    turn(3)
    out(0)
    table(2)
    out(1)
    table(3)
    out(2)
    out(3)
    for q in ("v", "s", "t", "g"):
        total[sem_of[q]] = cnt[sem_of[q]]
    for s in SEMAPHORES:
        if s in total:
            g.wait_ge(T.sem[s], total[s])
